import numpy as np
import ml_dtypes


def mxq(x, axis, fmt="e4m3"):
    dtype, down = {"e4m3": (ml_dtypes.float8_e4m3fn, 7), "e5m2": (ml_dtypes.float8_e5m2, 14)}[fmt]
    v = np.moveaxis(np.asarray(x, np.float32).astype(ml_dtypes.bfloat16).astype(np.float64), axis, -1)
    blocks = v.reshape(v.shape[:-1] + (-1, 32))
    amax = np.abs(blocks).max(-1, keepdims=True)
    byte = np.maximum(np.where(amax > 0, np.frexp(amax)[1] - 1 + 127, 0) - down, 1)
    scale = np.exp2(byte - 127.0)
    codes = (blocks / scale).astype(np.float32).astype(dtype).astype(np.float64)
    return np.moveaxis((codes * scale).reshape(v.shape), -1, axis)


WIDE = False


def mx_kscale(k):
    if not WIDE:
        return np.ones(k)
    levels = np.array([10, -10, 5, -5, 0])
    if k % 512:
        return np.exp2(np.random.permutation(np.resize(levels, k // 32))).repeat(32)
    a = np.empty((k // 512, 16))
    for p in range(k // 512):
        a[p, :8] = np.random.permutation(np.resize(levels, 8))
        for g in range(8):
            far = levels[np.abs(levels - a[p, g]) >= 10]
            a[p, g + 8] = far[np.random.randint(len(far))]
    return np.exp2(a.ravel()).repeat(32)


BF16 = ml_dtypes.bfloat16


def bf(x):
    return np.asarray(x, np.float32).astype(BF16)


def f64(x):
    return np.asarray(x).astype(np.float64)


NB, T, D, N, TWO = 128, 8, 1024, 1024, 2


def draw0():
    s, t = mx_kscale(D), mx_kscale(N)
    return {"u": bf(np.random.standard_normal((NB, T, D)) * s),
            "b": bf(np.random.standard_normal((TWO, D, N)) / np.sqrt(D) / s[None, :, None]),
            "nu": bf(np.random.uniform(-2.0, 0.0, N)),
            "theta": bf(np.random.uniform(0.0, 3.0, N)),
            "gamma": bf(np.random.uniform(0.5, 1.0, N) * t),
            "c": bf(np.random.standard_normal((TWO, N, D)) / np.sqrt(N) / t[None, :, None]),
            "d": bf(np.random.standard_normal(D) * 0.5 / s)}


def diagonal_eigenvalues(nu, theta):
    m = np.exp(-np.exp(nu))
    return m * np.cos(theta), m * np.sin(theta)


def core(u, b, nu, theta, gamma, c, d):
    u, b, nu, theta, gamma, c, d = f64(u), f64(b), f64(nu), f64(theta), f64(gamma), f64(c), f64(d)
    uq = mxq(u, 2, "e4m3")
    ar = uq @ mxq(b[0], 0, "e4m3")
    ai = uq @ mxq(b[1], 0, "e4m3")
    ar = ar * gamma
    ai = ai * gamma

    lr, li = diagonal_eigenvalues(nu, theta)

    hr = np.zeros((u.shape[0], nu.shape[0]))
    hi = np.zeros((u.shape[0], nu.shape[0]))
    real_states = []
    imag_states = []
    for step in range(T):
        hr_new = lr * hr - li * hi + ar[:, step]
        hi_new = lr * hi + li * hr + ai[:, step]
        real_states.append(hr_new)
        imag_states.append(hi_new)
        hr, hi = hr_new, hi_new
    hrs = np.stack(real_states, axis=1)
    his = np.stack(imag_states, axis=1)

    y = (mxq(hrs, 2, "e4m3") @ mxq(c[0], 0, "e4m3")) - (mxq(his, 2, "e4m3") @ mxq(c[1], 0, "e4m3"))

    y = y + d * u
    return y


def e4m3fn_bytes(y):
    return np.clip(np.asarray(y, np.float64), -448.0, 448.0).astype(np.float32).astype(ml_dtypes.float8_e4m3fn).view(np.uint8)


def e4m3fn_values(b):
    return np.asarray(b, np.uint8).view(ml_dtypes.float8_e4m3fn).astype(np.float64)


def setup_inputs():
    d = draw0()
    x0 = np.asarray(d['c']).astype(np.float64)
    s = (np.max(np.abs(x0), axis=(0, 2), keepdims=True) / 448.0).astype(np.float32)
    out = {}
    for k, v in d.items():
        if k == 'c':
            out['c_bytes'] = e4m3fn_bytes(x0 / s.astype(np.float64))
            out['c_scale'] = s
        else:
            out[k] = v
    return out


def reference(u, b, nu, theta, gamma, c_bytes, c_scale, d):
    return core(u, b, nu, theta, gamma, e4m3fn_values(c_bytes) * c_scale.astype(np.float64), d)

@@ -1,0 +1,365 @@
+import math
+from contextlib import ExitStack
+
+import concourse.mybir as mybir
+from concourse.masks import make_identity
+
+NB, T, D, N = 128, 8, 1024, 1024
+FLOPS = 2 * (NB * T) * D * (2 * N) + 2 * (NB * T) * (2 * N) * D
+
+F32 = mybir.dt.float32
+BF16 = mybir.dt.bfloat16
+U32 = mybir.dt.uint32
+U8 = mybir.dt.uint8
+FP8 = mybir.dt.float8_e4m3fn
+FP8X4 = mybir.dt.float8_e4m3fn_x4
+ACT = mybir.ActivationFunctionType
+ALU = mybir.AluOpType
+
+P = 128
+PACK = 4
+KP = P * PACK
+HALVES = 2
+PARTS = 2
+PAIR = 2
+RUN = 4
+
+
+def tile_linearrecurrentunitcomplexeightstep_kernel(tc, u, b, nu, theta, gamma, c_bytes, c_scale, d, out):
+    nc = tc.nc
+    with ExitStack() as ctx:
+        const = ctx.enter_context(tc.tile_pool(name="const", bufs=1))
+        work = ctx.enter_context(tc.tile_pool(name="work", bufs=1))
+        psum = ctx.enter_context(tc.psum_pool(name="psum", bufs=1))
+        ctx.enter_context(tc.manual_schedule())
+
+        def load_vector(queue, name, vec, dtype):
+            tile = const.tile([P, HALVES, PACK], dtype, name=name)
+            queue.dma_start(out=tile[:], in_=vec.rearrange("(g p j) -> p g j", p=P, j=PACK))
+            return tile[:].rearrange("p g j -> p (g j)")
+
+        b_raw, c_raw, u_raw = {}, {}, {}
+
+        def load_b(g, part, kh):
+            tile = work.tile([P, PACK, KP], BF16, name="b_raw", bufs=4)
+            rows = b[part, kh * KP:(kh + 1) * KP, g * KP:(g + 1) * KP]
+            nc.sync.dma_start(out=tile[:], in_=rows.rearrange("(p j) n -> p j n", j=PACK))
+            b_raw[g, part, kh] = tile
+
+        def load_c(g, part):
+            tile = work.tile([P, PACK, D], U8, name="c_raw", bufs=3)
+            rows = c_bytes[part, g * KP:(g + 1) * KP, :]
+            nc.sync.dma_start(out=tile[:], in_=rows.rearrange("(p j) f -> p j f", j=PACK))
+            c_raw[g, part] = tile
+
+        def load_u(pair):
+            tile = work.tile([P, PAIR, D], BF16, name="u_raw", bufs=2)
+            nc.sync.dma_start(out=tile[:], in_=u[:, PAIR * pair:PAIR * (pair + 1), :])
+            u_raw[pair] = tile
+
+        nu_sb = load_vector(nc.scalar, "nu_sb", nu, BF16)
+        theta_sb = load_vector(nc.scalar, "theta_sb", theta, BF16)
+        d_sb = load_vector(nc.scalar, "d_sb", d, BF16)
+        load_b(0, 0, 0)
+        load_b(0, 0, 1)
+        cs_sb = load_vector(nc.sync, "cs_sb", c_scale.rearrange("o n z -> (o n z)"), F32)
+        load_c(0, 0)
+        load_b(0, 1, 0)
+        load_u(0)
+        load_b(0, 1, 1)
+        gamma_sb = load_vector(nc.sync, "gamma_sb", gamma, BF16)
+        load_c(0, 1)
+        load_u(1)
+
+        ident = const.tile([P, P], F32, name="ident")
+        make_identity(nc, ident[:])
+
+        cols = HALVES * PACK
+        angle = const.tile([P, 2, cols], F32, name="angle")
+        nc.vector.tensor_copy(out=angle[:, 0, :], in_=theta_sb)
+        nc.vector.tensor_scalar(out=angle[:, 1, :], in0=theta_sb, scalar1=-1.0, scalar2=math.pi / 2,
+                                op0=ALU.mult, op1=ALU.add)
+        d_diag = const.tile([P, cols, P], BF16, name="d_diag")
+        nc.vector.tensor_tensor(out=d_diag[:], in0=ident[:].unsqueeze(1).to_broadcast([P, cols, P]),
+                                in1=d_sb.unsqueeze(2).to_broadcast([P, cols, P]), op=ALU.mult)
+        rate = const.tile([P, cols], F32, name="rate")
+        nc.scalar.activation(out=rate[:], in_=nu_sb, func=ACT.Exp)
+        modulus = const.tile([P, cols], F32, name="modulus")
+        nc.scalar.activation(out=modulus[:], in_=rate[:], func=ACT.Exp, scale=-1.0)
+        trig = const.tile([P, 2, cols], F32, name="trig")
+        nc.scalar.activation(out=trig[:], in_=angle[:], func=ACT.Sin)
+        cs_neg = const.tile([P, cols], F32, name="cs_neg")
+        nc.scalar.activation(out=cs_neg[:], in_=cs_sb, func=ACT.Copy, scale=-1.0)
+        c_factor = (cs_sb, cs_neg[:])
+        lam = const.tile([P, 2, cols], F32, name="lam")
+        li_neg = const.tile([P, cols], F32, name="li_neg")
+        gain = const.tile([P, cols], F32, name="gain")
+
+        def eigenvalues():
+            nc.vector.tensor_tensor(out=lam[:], in0=trig[:], in1=modulus[:].unsqueeze(1).to_broadcast([P, 2, cols]),
+                                    op=ALU.mult)
+            nc.vector.scalar_tensor_tensor(out=li_neg[:], in0=trig[:, 0, :], scalar=-1.0, in1=modulus[:],
+                                           op0=ALU.mult, op1=ALU.mult)
+
+        def mx_tiles(name, width, bufs):
+            codes = work.tile([P, width], U32, name=name + "_codes", bufs=bufs, align_bytes=64)
+            scales = work.tile([P, width], U8, name=name + "_scales", bufs=bufs, align_bytes=64)
+            return codes, scales
+
+        def quantize(name, bufs, grouped, width):
+            codes, scales = mx_tiles(name, width, bufs)
+            nc.vector.quantize_mx(out=codes[:].bitcast(FP8X4), scales=scales[:], in_=grouped)
+            return codes, scales
+
+        def matmul_mx(acc, lhs, lhs_cols, rhs, rhs_cols, start, stop):
+            nc.tensor.matmul_mx(out=acc, lhsT=lhs[0][:, lhs_cols].bitcast(FP8X4), lhsT_scale=lhs[1][:, lhs_cols],
+                                rhs=rhs[0][:, rhs_cols].bitcast(FP8X4), rhs_scale=rhs[1][:, rhs_cols],
+                                start=start, stop=stop)
+
+        def copy(on_scalar, dst, src):
+            if on_scalar:
+                nc.scalar.copy(out=dst, in_=src)
+            else:
+                nc.vector.tensor_copy(out=dst, in_=src)
+
+        c_wide, grouped, w_mx = {}, {}, {}
+
+        def widen_c(g, part, j):
+            if j == 0:
+                c_wide[g, part] = work.tile([P, PACK, D], BF16, name="c_wide", bufs=2)
+            col = PACK * g + j
+            nc.scalar.activation(out=c_wide[g, part][:, j, :], in_=c_raw[g, part][:, j, :].bitcast(FP8),
+                                 func=ACT.Copy, scale=c_factor[part][:, col:col + 1])
+
+        def interleave(unit, on_scalar):
+            kind, g, part, half = unit
+            tile = work.tile([P, KP * PACK], BF16, name="grouped", bufs=4, align_bytes=64)
+            if kind == "b":
+                src = b_raw[g, part, half][:].rearrange("p j (m s) -> p m j s", s=PACK)
+                dst = tile[:].rearrange("p (s m j) -> p m j s", s=PACK, j=PACK)
+            else:
+                src = c_wide[g, part][:, :, half * KP:(half + 1) * KP].rearrange("p j (c i) -> p c j i", i=RUN)
+                dst = tile[:].rearrange("p (c i j) -> p c j i", i=RUN, j=PACK)
+            copy(on_scalar, dst, src)
+            grouped[unit] = tile
+
+        def quantize_weights(unit):
+            w_mx[unit] = quantize("w", 16, grouped[unit][:], KP)
+
+        u_turned, u_mx = {}, {}
+
+        def turn_u(t):
+            pair, s = divmod(t, PAIR)
+            if s == 0:
+                u_turned[pair] = work.tile([P, HALVES, PAIR, NB * PACK], BF16, name="u_turned", bufs=4, align_bytes=64)
+            words = u_raw[pair][:, s, :].bitcast(F32)
+            bank = psum.tile([P, HALVES, 2, NB], F32, name="bank", bufs=8)
+            for kh in range(HALVES):
+                for w in range(2):
+                    nc.tensor.transpose(bank[:, kh, w, :], words[:, 2 * P * kh + w:2 * P * (kh + 1):2], ident[:])
+            dst = u_turned[pair][:, :, s, :].bitcast(F32).rearrange("p k (b w) -> p k b w", w=2)
+            nc.scalar.copy(out=dst, in_=bank[:].rearrange("p k w b -> p k b w"))
+
+        def quantize_u(pair):
+            u_mx[pair] = quantize("u", 4, u_turned[pair][:].rearrange("p k s x -> p (k s x)"), HALVES * PAIR * NB)
+
+        state, h_grouped, h_mx = {}, {}, {}
+
+        def project_in(g, pair, j):
+            if j == 0:
+                state[g, pair] = work.tile([P, PACK, PAIR, PARTS * NB], F32, name="state", bufs=7)
+            bank = psum.tile([P, PARTS, PAIR * NB], F32, name="bank", bufs=8)
+            for part in range(PARTS):
+                for kh in range(HALVES):
+                    matmul_mx(bank[:, part, :], w_mx["b", g, part, kh], slice(j * P, (j + 1) * P),
+                              u_mx[pair], slice(kh * PAIR * NB, (kh + 1) * PAIR * NB), kh == 0, kh == HALVES - 1)
+            col = PACK * g + j
+            nc.scalar.activation(out=state[g, pair][:, j].rearrange("p s (r b) -> p s r b", r=PARTS),
+                                 in_=bank[:].rearrange("p r (s b) -> p s r b", s=PAIR),
+                                 func=ACT.Copy, scale=gain[:, col:col + 1])
+
+        def step_view(g, t):
+            pair, s = divmod(t, PAIR)
+            return state[g, pair][:, :, s, :]
+
+        def recur(g, t, terms=range(3)):
+            old, new = step_view(g, t - 1), step_view(g, t)
+            re, im = slice(0, NB), slice(NB, 2 * NB)
+            table = ((slice(0, 2 * NB), slice(0, 2 * NB), lam[:, 1, :]), (re, im, li_neg[:]), (im, re, lam[:, 0, :]))
+            for term in terms:
+                to, frm, factor = table[term]
+                for j in range(PACK):
+                    col = PACK * g + j
+                    nc.vector.scalar_tensor_tensor(out=new[:, j, to], in0=old[:, j, frm], scalar=factor[:, col:col + 1],
+                                                   in1=new[:, j, to], op0=ALU.mult, op1=ALU.add)
+
+        def round_state(g, t):
+            tile = work.tile([P, PARTS * NB * PACK], BF16, name="h_grouped", bufs=4, align_bytes=64)
+            nc.scalar.copy(out=tile[:].rearrange("p (c i j) -> p c j i", i=RUN, j=PACK),
+                           in_=step_view(g, t).rearrange("p j (c i) -> p c j i", i=RUN))
+            h_grouped[g, t] = tile
+
+        def quantize_state(g, t):
+            h_mx[g, t] = quantize("h", 6, h_grouped[g, t][:], PARTS * NB)
+
+        result, acc_out = {}, {}
+
+        def skip_term(t, half):
+            pair, s = divmod(t, PAIR)
+            bank = psum.tile([P, PACK, P], F32, name="bank", bufs=8)
+            rows = u_turned[pair][:, half, s, :].rearrange("p (b j) -> p j b", j=PACK)
+            for j in range(PACK):
+                nc.tensor.matmul(bank[:, j, :], lhsT=rows[:, j, :], rhs=d_diag[:, PACK * half + j, :],
+                                 start=True, stop=True)
+            tile = work.tile([P, KP], F32, name="result", bufs=8)
+            nc.scalar.copy(out=tile[:].rearrange("p (m j) -> p m j", j=PACK), in_=bank[:].rearrange("p j m -> p m j"))
+            result[t, half] = tile
+
+        def project_out(t, groups):
+            for half in range(HALVES if 0 in groups else 0):
+                acc_out[t, half] = psum.tile([P, KP], F32, name="bank", bufs=8)
+            for g in groups:
+                for part in range(PARTS):
+                    for half in range(HALVES):
+                        matmul_mx(acc_out[t, half][:], h_mx[g, t], slice(part * NB, (part + 1) * NB),
+                                  w_mx["c", g, part, half], slice(0, KP),
+                                  g == 0 and part == 0, g == HALVES - 1 and part == PARTS - 1)
+
+        def finish(t, half):
+            tile = result[t, half]
+            nc.vector.tensor_tensor(out=tile[:], in0=acc_out[t, half][:], in1=tile[:], op=ALU.add)
+            nc.sync.dma_start(out=out[:, t, half * KP:(half + 1) * KP], in_=tile[:])
+
+        b_units = [("b", g, part, kh) for g in range(HALVES) for part in range(PARTS) for kh in range(HALVES)]
+        c_tiles = [(g, part) for g in range(HALVES) for part in range(PARTS)]
+        c_units = [("c", g, part, half) for g, part in c_tiles for half in range(HALVES)]
+        pending = []
+
+        def prepare(unit, on_scalar=False):
+            interleave(unit, on_scalar)
+            flush()
+            pending.append(unit)
+
+        def flush():
+            for unit in pending:
+                quantize_weights(unit)
+            pending.clear()
+
+        def widen_tile(k):
+            for j in range(PACK):
+                widen_c(*c_tiles[k], j)
+
+        def project_pair(g, pair):
+            for j in range(PACK):
+                project_in(g, pair, j)
+
+        def turn_pair(pair):
+            for s in range(PAIR):
+                turn_u(PAIR * pair + s)
+
+        prepare(b_units[0])
+        flush()
+        prepare(b_units[1])
+        widen_tile(0)
+        prepare(b_units[2])
+        turn_pair(0)
+        nc.scalar.copy(out=gain[:], in_=gamma_sb)
+        prepare(b_units[3])
+        load_c(1, 0)
+        load_b(1, 0, 0)
+        load_c(1, 1)
+        load_u(2)
+        widen_tile(1)
+        eigenvalues()
+        prepare(c_units[0])
+        quantize_u(0)
+        prepare(c_units[1])
+        project_pair(0, 0)
+        load_b(1, 0, 1)
+        load_b(1, 1, 0)
+        load_b(1, 1, 1)
+        turn_pair(1)
+        load_u(3)
+        widen_tile(2)
+        prepare(c_units[2])
+        prepare(c_units[3])
+        quantize_u(1)
+        recur(0, 1)
+        project_pair(0, 1)
+        widen_tile(3)
+        prepare(b_units[4])
+        prepare(c_units[4])
+        prepare(c_units[5])
+        turn_pair(2)
+        recur(0, 2)
+        prepare(c_units[6])
+        interleave(b_units[5], True)
+        quantize_u(2)
+        prepare(c_units[7])
+        project_pair(0, 2)
+        prepare(b_units[7])
+        quantize_weights(b_units[5])
+        interleave(b_units[6], True)
+        recur(0, 3)
+        flush()
+        quantize_weights(b_units[6])
+        turn_pair(3)
+        round_state(0, 0)
+        project_pair(1, 0)
+        quantize_u(3)
+        recur(0, 4)
+        project_pair(0, 3)
+        round_state(0, 1)
+        recur(0, 5)
+
+        quantize_state(0, 0)
+
+        last = T - 1
+        for t in range(last):
+            if t > 0:
+                recur(1, t)
+            if t < T - PAIR:
+                for j in range(2 * (t % 2), 2 * (t % 2) + 2):
+                    project_in(1, t // PAIR + 1, j)
+            round_state(1, t)
+            if t + 2 < T:
+                round_state(0, t + 2)
+            for half in range(HALVES):
+                skip_term(t, half)
+            if t in (0, 1):
+                recur(0, T - 2 + t)
+            quantize_state(0, t + 1)
+            if t >= 1:
+                quantize_state(1, t - 1)
+            if t >= 2:
+                for half in range(HALVES):
+                    finish(t - 2, half)
+            if t >= 1:
+                project_out(t - 1, range(HALVES))
+
+        for half in range(HALVES):
+            skip_term(last, half)
+        project_out(last - 1, [0])
+        finish(last - 2, 0)
+        recur(1, last, terms=[0])
+        quantize_state(1, last - 1)
+        recur(1, last, terms=[1, 2])
+        project_out(last, [0])
+        project_out(last - 1, [1])
+        tile = work.tile([P, PARTS * NB * PACK], BF16, name="h_grouped", bufs=4, align_bytes=64)
+        codes, scales = mx_tiles("h", PARTS * NB, 6)
+        h_mx[1, last] = codes, scales
+        for part in range(PARTS):
+            words = slice(part * NB, (part + 1) * NB)
+            dst = tile[:, part * KP:(part + 1) * KP]
+            copy(part == 0, dst.rearrange("p (c i j) -> p c j i", i=RUN, j=PACK),
+                 step_view(1, last)[:, :, words].rearrange("p j (c i) -> p c j i", i=RUN))
+        for part in range(PARTS):
+            words = slice(part * NB, (part + 1) * NB)
+            nc.vector.quantize_mx(out=codes[:, words].bitcast(FP8X4), scales=scales[:, words],
+                                  in_=tile[:, part * KP:(part + 1) * KP])
+        finish(last - 2, 1)
+        project_out(last, [1])
+        for t in (last - 1, last):
+            for half in range(HALVES):
+                finish(t, half)

@@ -23,6 +23,8 @@ HALVES = 2
 PARTS = 2
 PAIR = 2
 RUN = 4
+TENSOR_STEPS = 3
+SCALAR_UNITS = (4,)
 
 
 def tile_linearrecurrentunitcomplexeightstep_kernel(tc, u, b, nu, theta, gamma, c_bytes, c_scale, d, out):
@@ -31,7 +33,6 @@ def tile_linearrecurrentunitcomplexeightstep_kernel(tc, u, b, nu, theta, gamma, 
         const = ctx.enter_context(tc.tile_pool(name="const", bufs=1))
         work = ctx.enter_context(tc.tile_pool(name="work", bufs=1))
         psum = ctx.enter_context(tc.psum_pool(name="psum", bufs=1))
-        ctx.enter_context(tc.manual_schedule())
 
         def load_vector(queue, name, vec, dtype):
             tile = const.tile([P, HALVES, PACK], dtype, name=name)
@@ -57,37 +58,35 @@ def tile_linearrecurrentunitcomplexeightstep_kernel(tc, u, b, nu, theta, gamma, 
             nc.sync.dma_start(out=tile[:], in_=u[:, PAIR * pair:PAIR * (pair + 1), :])
             u_raw[pair] = tile
 
+        d_sb = load_vector(nc.sync, "d_sb", d, BF16)
+        load_b(0, 0, 0)
         nu_sb = load_vector(nc.scalar, "nu_sb", nu, BF16)
         theta_sb = load_vector(nc.scalar, "theta_sb", theta, BF16)
-        d_sb = load_vector(nc.scalar, "d_sb", d, BF16)
-        load_b(0, 0, 0)
-        load_b(0, 0, 1)
-        cs_sb = load_vector(nc.sync, "cs_sb", c_scale.rearrange("o n z -> (o n z)"), F32)
+        cs_sb = load_vector(nc.scalar, "cs_sb", c_scale.rearrange("o n z -> (o n z)"), F32)
         load_c(0, 0)
+        load_b(0, 0, 1)
         load_b(0, 1, 0)
         load_u(0)
         load_b(0, 1, 1)
         gamma_sb = load_vector(nc.sync, "gamma_sb", gamma, BF16)
-        load_c(0, 1)
         load_u(1)
+        load_c(0, 1)
 
         ident = const.tile([P, P], F32, name="ident")
         make_identity(nc, ident[:])
 
         cols = HALVES * PACK
-        angle = const.tile([P, 2, cols], F32, name="angle")
-        nc.vector.tensor_copy(out=angle[:, 0, :], in_=theta_sb)
-        nc.vector.tensor_scalar(out=angle[:, 1, :], in0=theta_sb, scalar1=-1.0, scalar2=math.pi / 2,
-                                op0=ALU.mult, op1=ALU.add)
         d_diag = const.tile([P, cols, P], BF16, name="d_diag")
         nc.vector.tensor_tensor(out=d_diag[:], in0=ident[:].unsqueeze(1).to_broadcast([P, cols, P]),
                                 in1=d_sb.unsqueeze(2).to_broadcast([P, cols, P]), op=ALU.mult)
         rate = const.tile([P, cols], F32, name="rate")
-        nc.scalar.activation(out=rate[:], in_=nu_sb, func=ACT.Exp)
         modulus = const.tile([P, cols], F32, name="modulus")
-        nc.scalar.activation(out=modulus[:], in_=rate[:], func=ACT.Exp, scale=-1.0)
         trig = const.tile([P, 2, cols], F32, name="trig")
-        nc.scalar.activation(out=trig[:], in_=angle[:], func=ACT.Sin)
+        with tc.manual_schedule(engines={mybir.EngineType.Activation}):
+            nc.scalar.activation(out=rate[:], in_=nu_sb, func=ACT.Exp)
+            nc.scalar.activation(out=modulus[:], in_=rate[:], func=ACT.Exp, scale=-1.0)
+            nc.scalar.activation(out=trig[:, 0, :], in_=theta_sb, func=ACT.Sin)
+            nc.scalar.activation(out=trig[:, 1, :], in_=theta_sb, func=ACT.Sin, scale=-1.0, bias=math.pi / 2)
         cs_neg = const.tile([P, cols], F32, name="cs_neg")
         nc.scalar.activation(out=cs_neg[:], in_=cs_sb, func=ACT.Copy, scale=-1.0)
         c_factor = (cs_sb, cs_neg[:])
@@ -100,6 +99,14 @@ def tile_linearrecurrentunitcomplexeightstep_kernel(tc, u, b, nu, theta, gamma, 
                                     op=ALU.mult)
             nc.vector.scalar_tensor_tensor(out=li_neg[:], in0=trig[:, 0, :], scalar=-1.0, in1=modulus[:],
                                            op0=ALU.mult, op1=ALU.mult)
+
+        cross = const.tile([P, PARTS, PACK, P], F32, name="cross")
+
+        def cross_matrices():
+            for part, factor in enumerate((li_neg[:], lam[:, 0, :])):
+                for j in range(PACK):
+                    nc.vector.tensor_scalar(out=cross[:, part, j, :], in0=ident[:], scalar1=factor[:, j:j + 1],
+                                            scalar2=None, op0=ALU.mult)
 
         def mx_tiles(name, width, bufs):
             codes = work.tile([P, width], U32, name=name + "_codes", bufs=bufs, align_bytes=64)
@@ -193,6 +200,25 @@ def tile_linearrecurrentunitcomplexeightstep_kernel(tc, u, b, nu, theta, gamma, 
                     nc.vector.scalar_tensor_tensor(out=new[:, j, to], in0=old[:, j, frm], scalar=factor[:, col:col + 1],
                                                    in1=new[:, j, to], op0=ALU.mult, op1=ALU.add)
 
+        def recur_on_tensor(t, js):
+            old, new = step_view(0, t - 1), step_view(0, t)
+            banks = []
+            for j in js:
+                bank = psum.tile([P, PARTS * NB], F32, name="bank", bufs=8)
+                nc.tensor.matmul(bank[:], lhsT=ident[:], rhs=new[:, j, :], start=True, stop=False)
+                for part in range(PARTS):
+                    other = 1 - part
+                    nc.tensor.matmul(bank[:, part * NB:(part + 1) * NB], lhsT=cross[:, part, j, :],
+                                     rhs=old[:, j, other * NB:(other + 1) * NB], start=False, stop=part == PARTS - 1)
+                banks.append(bank)
+            return banks
+
+        def update(t, js, banks):
+            old, new = step_view(0, t - 1), step_view(0, t)
+            for j, bank in zip(js, banks):
+                nc.vector.scalar_tensor_tensor(out=new[:, j, :], in0=old[:, j, :], scalar=lam[:, 1, j:j + 1],
+                                               in1=bank[:], op0=ALU.mult, op1=ALU.add)
+
         def round_state(g, t):
             tile = work.tile([P, PARTS * NB * PACK], BF16, name="h_grouped", bufs=4, align_bytes=64)
             nc.scalar.copy(out=tile[:].rearrange("p (c i j) -> p c j i", i=RUN, j=PACK),
@@ -257,77 +283,79 @@ def tile_linearrecurrentunitcomplexeightstep_kernel(tc, u, b, nu, theta, gamma, 
             for s in range(PAIR):
                 turn_u(PAIR * pair + s)
 
+        def step_first_half(t):
+            if t <= TENSOR_STEPS:
+                update(t, range(PACK), recur_on_tensor(t, range(PACK)))
+            else:
+                recur(0, t)
+
         prepare(b_units[0])
-        flush()
+        eigenvalues()
         prepare(b_units[1])
-        widen_tile(0)
-        prepare(b_units[2])
         turn_pair(0)
+        prepare(b_units[2])
         nc.scalar.copy(out=gain[:], in_=gamma_sb)
         prepare(b_units[3])
-        load_c(1, 0)
-        load_b(1, 0, 0)
-        load_c(1, 1)
-        load_u(2)
-        widen_tile(1)
-        eigenvalues()
-        prepare(c_units[0])
         quantize_u(0)
-        prepare(c_units[1])
+        flush()
+        cross_matrices()
         project_pair(0, 0)
+        load_b(1, 0, 0)
         load_b(1, 0, 1)
+        load_c(1, 0)
+        load_u(2)
+        turn_pair(1)
+        quantize_u(1)
+        step_first_half(1)
+        project_pair(0, 1)
+        step_first_half(2)
+        step_first_half(3)
+        widen_tile(0)
+        prepare(c_units[0])
+        prepare(c_units[1])
         load_b(1, 1, 0)
         load_b(1, 1, 1)
-        turn_pair(1)
+        load_c(1, 1)
         load_u(3)
-        widen_tile(2)
-        prepare(c_units[2])
-        prepare(c_units[3])
-        quantize_u(1)
-        recur(0, 1)
-        project_pair(0, 1)
-        widen_tile(3)
-        prepare(b_units[4])
-        prepare(c_units[4])
-        prepare(c_units[5])
         turn_pair(2)
-        recur(0, 2)
-        prepare(c_units[6])
-        interleave(b_units[5], True)
         quantize_u(2)
-        prepare(c_units[7])
         project_pair(0, 2)
-        prepare(b_units[7])
-        quantize_weights(b_units[5])
-        interleave(b_units[6], True)
-        recur(0, 3)
+        step_first_half(4)
+        step_first_half(5)
+        widen_tile(1)
+        for unit in b_units[4:6] + c_units[2:4] + b_units[6:8]:
+            prepare(unit)
         flush()
-        quantize_weights(b_units[6])
-        turn_pair(3)
-        round_state(0, 0)
         project_pair(1, 0)
+        widen_tile(2)
+        prepare(c_units[4], 4 in SCALAR_UNITS)
+        prepare(c_units[5])
+        widen_tile(3)
+        prepare(c_units[6], 6 in SCALAR_UNITS)
+        prepare(c_units[7])
+        flush()
+        turn_pair(3)
         quantize_u(3)
-        recur(0, 4)
         project_pair(0, 3)
+        round_state(0, 0)
         round_state(0, 1)
-        recur(0, 5)
-
         quantize_state(0, 0)
 
         last = T - 1
         for t in range(last):
             if t > 0:
                 recur(1, t)
+            js = range(2 * (t % 2), 2 * (t % 2) + 2)
             if t < T - PAIR:
-                for j in range(2 * (t % 2), 2 * (t % 2) + 2):
+                for j in js:
                     project_in(1, t // PAIR + 1, j)
             round_state(1, t)
             if t + 2 < T:
                 round_state(0, t + 2)
             for half in range(HALVES):
                 skip_term(t, half)
-            if t in (0, 1):
-                recur(0, T - 2 + t)
+            if t < 2:
+                step_first_half(6 + t)
             quantize_state(0, t + 1)
             if t >= 1:
                 quantize_state(1, t - 1)

@@ -58,37 +58,43 @@ def tile_linearrecurrentunitcomplexeightstep_kernel(tc, u, b, nu, theta, gamma, 
             nc.sync.dma_start(out=tile[:], in_=u[:, PAIR * pair:PAIR * (pair + 1), :])
             u_raw[pair] = tile
 
-        d_sb = load_vector(nc.sync, "d_sb", d, BF16)
-        load_b(0, 0, 0)
+        first_b = []
+        for piece in range(2):
+            tile = work.tile([P, PACK, KP // 2], BF16, name="b_first", bufs=2)
+            rows = b[0, 0:KP, piece * KP // 2:(piece + 1) * KP // 2]
+            nc.sync.dma_start(out=tile[:], in_=rows.rearrange("(p j) n -> p j n", j=PACK))
+            first_b.append(tile)
+        d_sb = load_vector(nc.scalar, "d_sb", d, BF16)
         nu_sb = load_vector(nc.scalar, "nu_sb", nu, BF16)
         theta_sb = load_vector(nc.scalar, "theta_sb", theta, BF16)
         cs_sb = load_vector(nc.scalar, "cs_sb", c_scale.rearrange("o n z -> (o n z)"), F32)
-        load_c(0, 0)
         load_b(0, 0, 1)
-        load_b(0, 1, 0)
         load_u(0)
+        load_b(0, 1, 0)
         load_b(0, 1, 1)
-        gamma_sb = load_vector(nc.sync, "gamma_sb", gamma, BF16)
+        load_c(0, 0)
         load_u(1)
-        load_c(0, 1)
+        gamma_sb = load_vector(nc.sync, "gamma_sb", gamma, BF16)
 
         ident = const.tile([P, P], F32, name="ident")
         make_identity(nc, ident[:])
 
         cols = HALVES * PACK
         d_diag = const.tile([P, cols, P], BF16, name="d_diag")
-        nc.vector.tensor_tensor(out=d_diag[:], in0=ident[:].unsqueeze(1).to_broadcast([P, cols, P]),
-                                in1=d_sb.unsqueeze(2).to_broadcast([P, cols, P]), op=ALU.mult)
+        d_wide = const.tile([P, cols], F32, name="d_wide")
         rate = const.tile([P, cols], F32, name="rate")
         modulus = const.tile([P, cols], F32, name="modulus")
         trig = const.tile([P, 2, cols], F32, name="trig")
         with tc.manual_schedule(engines={mybir.EngineType.Activation}):
+            nc.scalar.copy(out=d_wide[:], in_=d_sb)
+            for col in range(cols):
+                nc.scalar.activation(out=d_diag[:, col, :], in_=ident[:], func=ACT.Copy, scale=d_wide[:, col:col + 1])
             nc.scalar.activation(out=rate[:], in_=nu_sb, func=ACT.Exp)
             nc.scalar.activation(out=modulus[:], in_=rate[:], func=ACT.Exp, scale=-1.0)
             nc.scalar.activation(out=trig[:, 0, :], in_=theta_sb, func=ACT.Sin)
             nc.scalar.activation(out=trig[:, 1, :], in_=theta_sb, func=ACT.Sin, scale=-1.0, bias=math.pi / 2)
+        ctx.enter_context(tc.manual_schedule(engines={mybir.EngineType.SP}))
         cs_neg = const.tile([P, cols], F32, name="cs_neg")
-        nc.scalar.activation(out=cs_neg[:], in_=cs_sb, func=ACT.Copy, scale=-1.0)
         c_factor = (cs_sb, cs_neg[:])
         lam = const.tile([P, 2, cols], F32, name="lam")
         li_neg = const.tile([P, cols], F32, name="li_neg")
@@ -133,7 +139,7 @@ def tile_linearrecurrentunitcomplexeightstep_kernel(tc, u, b, nu, theta, gamma, 
 
         def widen_c(g, part, j):
             if j == 0:
-                c_wide[g, part] = work.tile([P, PACK, D], BF16, name="c_wide", bufs=2)
+                c_wide[g, part] = work.tile([P, PACK, D], BF16, name="c_wide", bufs=3)
             col = PACK * g + j
             nc.scalar.activation(out=c_wide[g, part][:, j, :], in_=c_raw[g, part][:, j, :].bitcast(FP8),
                                  func=ACT.Copy, scale=c_factor[part][:, col:col + 1])
@@ -174,7 +180,7 @@ def tile_linearrecurrentunitcomplexeightstep_kernel(tc, u, b, nu, theta, gamma, 
 
         def project_in(g, pair, j):
             if j == 0:
-                state[g, pair] = work.tile([P, PACK, PAIR, PARTS * NB], F32, name="state", bufs=7)
+                state[g, pair] = work.tile([P, PACK, PAIR, PARTS * NB], F32, name="state", bufs=6)
             bank = psum.tile([P, PARTS, PAIR * NB], F32, name="bank", bufs=8)
             for part in range(PARTS):
                 for kh in range(HALVES):
@@ -251,10 +257,12 @@ def tile_linearrecurrentunitcomplexeightstep_kernel(tc, u, b, nu, theta, gamma, 
                                   w_mx["c", g, part, half], slice(0, KP),
                                   g == 0 and part == 0, g == HALVES - 1 and part == PARTS - 1)
 
-        def finish(t, half):
-            tile = result[t, half]
-            nc.vector.tensor_tensor(out=tile[:], in0=acc_out[t, half][:], in1=tile[:], op=ALU.add)
-            nc.sync.dma_start(out=out[:, t, half * KP:(half + 1) * KP], in_=tile[:])
+        def finish(t, half, pieces=1):
+            tile, width = result[t, half], KP // pieces
+            for piece in range(pieces):
+                span = slice(piece * width, (piece + 1) * width)
+                nc.vector.tensor_tensor(out=tile[:, span], in0=acc_out[t, half][:, span], in1=tile[:, span], op=ALU.add)
+                nc.sync.dma_start(out=out[:, t, half * KP:(half + 1) * KP][:, span], in_=tile[:, span])
 
         b_units = [("b", g, part, kh) for g in range(HALVES) for part in range(PARTS) for kh in range(HALVES)]
         c_tiles = [(g, part) for g in range(HALVES) for part in range(PARTS)]
@@ -283,94 +291,117 @@ def tile_linearrecurrentunitcomplexeightstep_kernel(tc, u, b, nu, theta, gamma, 
             for s in range(PAIR):
                 turn_u(PAIR * pair + s)
 
-        def step_first_half(t):
-            if t <= TENSOR_STEPS:
-                update(t, range(PACK), recur_on_tensor(t, range(PACK)))
-            else:
-                recur(0, t)
+        def skip_step(t):
+            for half in range(HALVES):
+                skip_term(t, half)
 
-        prepare(b_units[0])
-        eigenvalues()
-        prepare(b_units[1])
+        tile = work.tile([P, KP * PACK], BF16, name="grouped", bufs=4, align_bytes=64)
+        for piece in range(2):
+            nc.vector.tensor_copy(
+                out=tile[:].rearrange("p (s h m j) -> p h m j s", s=PACK, h=2, j=PACK)[:, piece],
+                in_=first_b[piece][:].rearrange("p j (m s) -> p m j s", s=PACK))
+        grouped[b_units[0]] = tile
+        quantize_weights(b_units[0])
         turn_pair(0)
+        prepare(b_units[1])
+        eigenvalues()
+        skip_step(0)
+        skip_step(1)
         prepare(b_units[2])
-        nc.scalar.copy(out=gain[:], in_=gamma_sb)
-        prepare(b_units[3])
-        quantize_u(0)
-        flush()
-        cross_matrices()
-        project_pair(0, 0)
         load_b(1, 0, 0)
         load_b(1, 0, 1)
+        quantize_u(0)
+        prepare(b_units[3])
+        load_b(1, 1, 0)
+        load_c(0, 1)
+        nc.scalar.copy(out=gain[:], in_=gamma_sb)
+        nc.scalar.activation(out=cs_neg[:], in_=cs_sb, func=ACT.Copy, scale=-1.0)
+        widen_c(0, 0, 0)
+        turn_pair(1)
+        cross_matrices()
+        flush()
+        load_b(1, 1, 1)
         load_c(1, 0)
         load_u(2)
-        turn_pair(1)
+        widen_c(0, 0, 1)
+        widen_c(0, 0, 2)
+        project_pair(0, 0)
         quantize_u(1)
-        step_first_half(1)
+        prepare(b_units[4])
         project_pair(0, 1)
-        step_first_half(2)
-        step_first_half(3)
-        widen_tile(0)
-        prepare(c_units[0])
-        prepare(c_units[1])
-        load_b(1, 1, 0)
-        load_b(1, 1, 1)
-        load_c(1, 1)
+        widen_c(0, 0, 3)
         load_u(3)
-        turn_pair(2)
-        quantize_u(2)
-        project_pair(0, 2)
-        step_first_half(4)
-        step_first_half(5)
-        widen_tile(1)
-        for unit in b_units[4:6] + c_units[2:4] + b_units[6:8]:
+        load_c(1, 1)
+        prepare(b_units[5])
+
+        later = b_units[6:8] + c_units[0:4]
+        extra = {
+            0: [lambda: widen_tile(1)],
+            2: [lambda: project_pair(1, 0), lambda: widen_tile(2)],
+            4: [lambda: turn_pair(2), lambda: widen_tile(3)],
+        }
+        waiting = None
+        for i, unit in enumerate(later):
+            t, js = 1 + i // 2, range(2 * (i % 2), 2 * (i % 2) + 2)
+            half_step = (t, js, recur_on_tensor(t, js))
             prepare(unit)
-        flush()
-        project_pair(1, 0)
-        widen_tile(2)
-        prepare(c_units[4], 4 in SCALAR_UNITS)
+            if waiting is not None:
+                update(*waiting)
+            waiting = half_step
+            for job in extra.get(i, []):
+                job()
+        prepare(c_units[4])
+        update(*waiting)
+        project_pair(1, 1)
         prepare(c_units[5])
-        widen_tile(3)
-        prepare(c_units[6], 6 in SCALAR_UNITS)
-        prepare(c_units[7])
-        flush()
-        turn_pair(3)
-        quantize_u(3)
-        project_pair(0, 3)
+        quantize_u(2)
+        interleave(c_units[7], True)
+        recur(1, 1)
         round_state(0, 0)
-        round_state(0, 1)
+        round_state(1, 0)
+        prepare(c_units[6])
+        project_pair(0, 2)
+        quantize_weights(c_units[7])
+        flush()
         quantize_state(0, 0)
+        quantize_state(1, 0)
+        turn_pair(3)
+        round_state(0, 1)
+        round_state(1, 1)
+        project_out(0, range(HALVES))
 
         last = T - 1
-        for t in range(last):
-            if t > 0:
-                recur(1, t)
+        for t in range(2, last):
+            recur(1, t)
+            if t == 2:
+                quantize_u(3)
             js = range(2 * (t % 2), 2 * (t % 2) + 2)
             if t < T - PAIR:
                 for j in js:
                     project_in(1, t // PAIR + 1, j)
+            if t < 4:
+                for j in js:
+                    project_in(0, 3, j)
+            quantize_state(0, t - 1)
+            quantize_state(1, t - 1)
+            round_state(0, t)
             round_state(1, t)
+            skip_step(t)
             if t + 2 < T:
-                round_state(0, t + 2)
+                recur(0, t + 2)
             for half in range(HALVES):
-                skip_term(t, half)
-            if t < 2:
-                step_first_half(6 + t)
-            quantize_state(0, t + 1)
-            if t >= 1:
-                quantize_state(1, t - 1)
-            if t >= 2:
-                for half in range(HALVES):
-                    finish(t - 2, half)
-            if t >= 1:
-                project_out(t - 1, range(HALVES))
+                finish(t - 2, half)
+            project_out(t - 1, range(HALVES))
 
+        round_state(0, last)
+        quantize_state(0, last - 1)
         for half in range(HALVES):
             skip_term(last, half)
         project_out(last - 1, [0])
         finish(last - 2, 0)
         recur(1, last, terms=[0])
         quantize_state(1, last - 1)
+        quantize_state(0, last)
         recur(1, last, terms=[1, 2])
         project_out(last, [0])
         project_out(last - 1, [1])
@@ -388,6 +419,7 @@ def tile_linearrecurrentunitcomplexeightstep_kernel(tc, u, b, nu, theta, gamma, 
                                   in_=tile[:, part * KP:(part + 1) * KP])
         finish(last - 2, 1)
         project_out(last, [1])
-        for t in (last - 1, last):
-            for half in range(HALVES):
-                finish(t, half)
+        for half in range(HALVES):
+            finish(last - 1, half)
+        finish(last, 0)
+        finish(last, 1, pieces=2)

@@ -18,13 +18,14 @@ ALU = mybir.AluOpType
 
 P = 128
 PACK = 4
-KP = P * PACK
-HALVES = 2
+SPAN = P * PACK
+SPANS = 2
 PARTS = 2
 PAIR = 2
 RUN = 4
-TENSOR_STEPS = 3
-SCALAR_UNITS = (4,)
+COLS = SPANS * PACK
+BANKS = 8
+LAST = T - 1
 
 
 def tile_linearrecurrentunitcomplexeightstep_kernel(tc, u, b, nu, theta, gamma, c_bytes, c_scale, d, out):
@@ -33,23 +34,24 @@ def tile_linearrecurrentunitcomplexeightstep_kernel(tc, u, b, nu, theta, gamma, 
         const = ctx.enter_context(tc.tile_pool(name="const", bufs=1))
         work = ctx.enter_context(tc.tile_pool(name="work", bufs=1))
         psum = ctx.enter_context(tc.psum_pool(name="psum", bufs=1))
-
-        def load_vector(queue, name, vec, dtype):
-            tile = const.tile([P, HALVES, PACK], dtype, name=name)
-            queue.dma_start(out=tile[:], in_=vec.rearrange("(g p j) -> p g j", p=P, j=PACK))
-            return tile[:].rearrange("p g j -> p (g j)")
+        ctx.enter_context(tc.manual_schedule())
 
         b_raw, c_raw, u_raw = {}, {}, {}
 
-        def load_b(g, part, kh):
-            tile = work.tile([P, PACK, KP], BF16, name="b_raw", bufs=4)
-            rows = b[part, kh * KP:(kh + 1) * KP, g * KP:(g + 1) * KP]
+        def load_vector(queue, name, vec, dtype):
+            tile = const.tile([P, SPANS, PACK], dtype, name=name)
+            queue.dma_start(out=tile[:], in_=vec.rearrange("(q p j) -> p q j", p=P, j=PACK))
+            return tile[:].rearrange("p q j -> p (q j)")
+
+        def load_b(g, part, q):
+            tile = work.tile([P, PACK, SPAN], BF16, name="b_raw", bufs=4)
+            rows = b[part, q * SPAN:(q + 1) * SPAN, g * SPAN:(g + 1) * SPAN]
             nc.sync.dma_start(out=tile[:], in_=rows.rearrange("(p j) n -> p j n", j=PACK))
-            b_raw[g, part, kh] = tile
+            b_raw[g, part, q] = tile
 
         def load_c(g, part):
             tile = work.tile([P, PACK, D], U8, name="c_raw", bufs=3)
-            rows = c_bytes[part, g * KP:(g + 1) * KP, :]
+            rows = c_bytes[part, g * SPAN:(g + 1) * SPAN, :]
             nc.sync.dma_start(out=tile[:], in_=rows.rearrange("(p j) f -> p j f", j=PACK))
             c_raw[g, part] = tile
 
@@ -58,368 +60,369 @@ def tile_linearrecurrentunitcomplexeightstep_kernel(tc, u, b, nu, theta, gamma, 
             nc.sync.dma_start(out=tile[:], in_=u[:, PAIR * pair:PAIR * (pair + 1), :])
             u_raw[pair] = tile
 
+        piece_cols = SPAN // 2
         first_b = []
         for piece in range(2):
-            tile = work.tile([P, PACK, KP // 2], BF16, name="b_first", bufs=2)
-            rows = b[0, 0:KP, piece * KP // 2:(piece + 1) * KP // 2]
-            nc.sync.dma_start(out=tile[:], in_=rows.rearrange("(p j) n -> p j n", j=PACK))
-            first_b.append(tile)
-        d_sb = load_vector(nc.scalar, "d_sb", d, BF16)
+            piece_tile = work.tile([P, PACK, piece_cols], BF16, name="b_first", bufs=2)
+            piece_rows = b[0, 0:SPAN, piece * piece_cols:(piece + 1) * piece_cols]
+            nc.sync.dma_start(out=piece_tile[:], in_=piece_rows.rearrange("(p j) n -> p j n", j=PACK))
+            first_b.append(piece_tile)
         nu_sb = load_vector(nc.scalar, "nu_sb", nu, BF16)
         theta_sb = load_vector(nc.scalar, "theta_sb", theta, BF16)
         cs_sb = load_vector(nc.scalar, "cs_sb", c_scale.rearrange("o n z -> (o n z)"), F32)
         load_b(0, 0, 1)
-        load_u(0)
-        load_b(0, 1, 0)
-        load_b(0, 1, 1)
         load_c(0, 0)
+        load_b(0, 1, 0)
+        load_u(0)
+        load_b(0, 1, 1)
         load_u(1)
         gamma_sb = load_vector(nc.sync, "gamma_sb", gamma, BF16)
+        d_sb = load_vector(nc.sync, "d_sb", d, BF16)
 
         ident = const.tile([P, P], F32, name="ident")
         make_identity(nc, ident[:])
 
-        cols = HALVES * PACK
-        d_diag = const.tile([P, cols, P], BF16, name="d_diag")
-        d_wide = const.tile([P, cols], F32, name="d_wide")
-        rate = const.tile([P, cols], F32, name="rate")
-        modulus = const.tile([P, cols], F32, name="modulus")
-        trig = const.tile([P, 2, cols], F32, name="trig")
-        with tc.manual_schedule(engines={mybir.EngineType.Activation}):
-            nc.scalar.copy(out=d_wide[:], in_=d_sb)
-            for col in range(cols):
-                nc.scalar.activation(out=d_diag[:, col, :], in_=ident[:], func=ACT.Copy, scale=d_wide[:, col:col + 1])
-            nc.scalar.activation(out=rate[:], in_=nu_sb, func=ACT.Exp)
-            nc.scalar.activation(out=modulus[:], in_=rate[:], func=ACT.Exp, scale=-1.0)
-            nc.scalar.activation(out=trig[:, 0, :], in_=theta_sb, func=ACT.Sin)
-            nc.scalar.activation(out=trig[:, 1, :], in_=theta_sb, func=ACT.Sin, scale=-1.0, bias=math.pi / 2)
-        ctx.enter_context(tc.manual_schedule(engines={mybir.EngineType.SP}))
-        cs_neg = const.tile([P, cols], F32, name="cs_neg")
-        c_factor = (cs_sb, cs_neg[:])
-        lam = const.tile([P, 2, cols], F32, name="lam")
-        li_neg = const.tile([P, cols], F32, name="li_neg")
-        gain = const.tile([P, cols], F32, name="gain")
+        rate = const.tile([P, COLS], F32, name="rate")
+        modulus = const.tile([P, COLS], F32, name="modulus")
+        sin_cos = const.tile([P, 2, COLS], F32, name="sin_cos")
+        li_lr = const.tile([P, 2, COLS], F32, name="li_lr")
+        li_neg = const.tile([P, COLS], F32, name="li_neg")
+        li, lr = li_lr[:, 0, :], li_lr[:, 1, :]
+        cross = const.tile([P, PARTS, PACK, P], F32, name="cross")
+        gain = const.tile([P, COLS], F32, name="gain")
+        cs_neg = const.tile([P, COLS], F32, name="cs_neg")
+        d_wide = const.tile([P, COLS], F32, name="d_wide")
+        d_diag = const.tile([P, COLS, P], BF16, name="d_diag")
+
+        nc.scalar.activation(out=rate[:], in_=nu_sb, func=ACT.Exp)
+        nc.scalar.activation(out=modulus[:], in_=rate[:], func=ACT.Exp, scale=-1.0)
+        nc.scalar.activation(out=sin_cos[:, 0, :], in_=theta_sb, func=ACT.Sin)
+        nc.scalar.activation(out=sin_cos[:, 1, :], in_=theta_sb, func=ACT.Sin, scale=-1.0, bias=math.pi / 2)
 
         def eigenvalues():
-            nc.vector.tensor_tensor(out=lam[:], in0=trig[:], in1=modulus[:].unsqueeze(1).to_broadcast([P, 2, cols]),
-                                    op=ALU.mult)
-            nc.vector.scalar_tensor_tensor(out=li_neg[:], in0=trig[:, 0, :], scalar=-1.0, in1=modulus[:],
+            nc.vector.tensor_tensor(out=li_lr[:], in0=sin_cos[:],
+                                    in1=modulus[:].unsqueeze(1).to_broadcast([P, 2, COLS]), op=ALU.mult)
+            nc.vector.scalar_tensor_tensor(out=li_neg[:], in0=sin_cos[:, 0, :], scalar=-1.0, in1=modulus[:],
                                            op0=ALU.mult, op1=ALU.mult)
 
-        cross = const.tile([P, PARTS, PACK, P], F32, name="cross")
-
         def cross_matrices():
-            for part, factor in enumerate((li_neg[:], lam[:, 0, :])):
+            for part, factor in enumerate((li_neg[:], li)):
                 for j in range(PACK):
                     nc.vector.tensor_scalar(out=cross[:, part, j, :], in0=ident[:], scalar1=factor[:, j:j + 1],
                                             scalar2=None, op0=ALU.mult)
+
+        def scalar_constants():
+            nc.scalar.copy(out=gain[:], in_=gamma_sb)
+            nc.scalar.activation(out=cs_neg[:], in_=cs_sb, func=ACT.Copy, scale=-1.0)
+            nc.scalar.copy(out=d_wide[:], in_=d_sb)
+            for col in range(COLS):
+                nc.scalar.activation(out=d_diag[:, col, :], in_=ident[:], func=ACT.Copy, scale=d_wide[:, col:col + 1])
 
         def mx_tiles(name, width, bufs):
             codes = work.tile([P, width], U32, name=name + "_codes", bufs=bufs, align_bytes=64)
             scales = work.tile([P, width], U8, name=name + "_scales", bufs=bufs, align_bytes=64)
             return codes, scales
 
-        def quantize(name, bufs, grouped, width):
-            codes, scales = mx_tiles(name, width, bufs)
-            nc.vector.quantize_mx(out=codes[:].bitcast(FP8X4), scales=scales[:], in_=grouped)
-            return codes, scales
+        def quantize(operand, cols, values):
+            codes, scales = operand
+            nc.vector.quantize_mx(out=codes[:, cols].bitcast(FP8X4), scales=scales[:, cols], in_=values)
 
         def matmul_mx(acc, lhs, lhs_cols, rhs, rhs_cols, start, stop):
             nc.tensor.matmul_mx(out=acc, lhsT=lhs[0][:, lhs_cols].bitcast(FP8X4), lhsT_scale=lhs[1][:, lhs_cols],
                                 rhs=rhs[0][:, rhs_cols].bitcast(FP8X4), rhs_scale=rhs[1][:, rhs_cols],
                                 start=start, stop=stop)
 
-        def copy(on_scalar, dst, src):
-            if on_scalar:
-                nc.scalar.copy(out=dst, in_=src)
-            else:
-                nc.vector.tensor_copy(out=dst, in_=src)
+        def interleave_views(dst, src):
+            return (dst.rearrange("p (c i j) -> p c j i", i=RUN, j=PACK),
+                    src.rearrange("p j (c i) -> p c j i", i=RUN))
 
-        c_wide, grouped, w_mx = {}, {}, {}
+        b_blocks = [("b", g, part, q) for g in range(SPANS) for part in range(PARTS) for q in range(SPANS)]
+        c_blocks = [("c", g, part, q) for g in range(SPANS) for part in range(PARTS) for q in range(SPANS)]
+        c_wide, w_values, w_mx, unquantized = {}, {}, {}, []
 
-        def widen_c(g, part, j):
-            if j == 0:
-                c_wide[g, part] = work.tile([P, PACK, D], BF16, name="c_wide", bufs=3)
-            col = PACK * g + j
-            nc.scalar.activation(out=c_wide[g, part][:, j, :], in_=c_raw[g, part][:, j, :].bitcast(FP8),
-                                 func=ACT.Copy, scale=c_factor[part][:, col:col + 1])
+        def widen_c(g, part):
+            tile = work.tile([P, PACK, D], BF16, name="c_wide", bufs=3)
+            factor = (cs_sb, cs_neg[:])[part]
+            for j in range(PACK):
+                col = PACK * g + j
+                nc.scalar.activation(out=tile[:, j, :], in_=c_raw[g, part][:, j, :].bitcast(FP8),
+                                     func=ACT.Copy, scale=factor[:, col:col + 1])
+            c_wide[g, part] = tile
 
-        def interleave(unit, on_scalar):
-            kind, g, part, half = unit
-            tile = work.tile([P, KP * PACK], BF16, name="grouped", bufs=4, align_bytes=64)
+        def values_tile(block):
+            w_values[block] = work.tile([P, SPAN * PACK], BF16, name="w_values", bufs=4, align_bytes=64)
+            return w_values[block]
+
+        def interleave(block):
+            kind, g, part, q = block
+            tile = values_tile(block)
             if kind == "b":
-                src = b_raw[g, part, half][:].rearrange("p j (m s) -> p m j s", s=PACK)
                 dst = tile[:].rearrange("p (s m j) -> p m j s", s=PACK, j=PACK)
+                src = b_raw[g, part, q][:].rearrange("p j (m s) -> p m j s", s=PACK)
             else:
-                src = c_wide[g, part][:, :, half * KP:(half + 1) * KP].rearrange("p j (c i) -> p c j i", i=RUN)
-                dst = tile[:].rearrange("p (c i j) -> p c j i", i=RUN, j=PACK)
-            copy(on_scalar, dst, src)
-            grouped[unit] = tile
+                dst, src = interleave_views(tile[:], c_wide[g, part][:, :, q * SPAN:(q + 1) * SPAN])
+            nc.vector.tensor_copy(out=dst, in_=src)
 
-        def quantize_weights(unit):
-            w_mx[unit] = quantize("w", 16, grouped[unit][:], KP)
+        def quantize_block(block):
+            w_mx[block] = mx_tiles("w", SPAN, len(b_blocks) + len(c_blocks))
+            quantize(w_mx[block], slice(0, SPAN), w_values[block][:])
+
+        def quantize_waiting():
+            for block in unquantized:
+                quantize_block(block)
+            unquantized.clear()
+
+        def prepare(block):
+            interleave(block)
+            quantize_waiting()
+            unquantized.append(block)
 
         u_turned, u_mx = {}, {}
 
-        def turn_u(t):
-            pair, s = divmod(t, PAIR)
-            if s == 0:
-                u_turned[pair] = work.tile([P, HALVES, PAIR, NB * PACK], BF16, name="u_turned", bufs=4, align_bytes=64)
-            words = u_raw[pair][:, s, :].bitcast(F32)
-            bank = psum.tile([P, HALVES, 2, NB], F32, name="bank", bufs=8)
-            for kh in range(HALVES):
-                for w in range(2):
-                    nc.tensor.transpose(bank[:, kh, w, :], words[:, 2 * P * kh + w:2 * P * (kh + 1):2], ident[:])
-            dst = u_turned[pair][:, :, s, :].bitcast(F32).rearrange("p k (b w) -> p k b w", w=2)
-            nc.scalar.copy(out=dst, in_=bank[:].rearrange("p k w b -> p k b w"))
+        def turn_u(pair):
+            tile = work.tile([P, SPANS, PAIR, NB * PACK], BF16, name="u_turned", bufs=T // PAIR, align_bytes=64)
+            for s in range(PAIR):
+                words = u_raw[pair][:, s, :].bitcast(F32)
+                bank = psum.tile([P, SPANS, 2, NB], F32, name="bank", bufs=BANKS)
+                for q in range(SPANS):
+                    for w in range(2):
+                        nc.tensor.transpose(bank[:, q, w, :], words[:, 2 * P * q + w:2 * P * (q + 1):2], ident[:])
+                nc.scalar.copy(out=tile[:, :, s, :].bitcast(F32).rearrange("p q (r w) -> p q r w", w=2),
+                               in_=bank[:].rearrange("p q w r -> p q r w"))
+            u_turned[pair] = tile
 
         def quantize_u(pair):
-            u_mx[pair] = quantize("u", 4, u_turned[pair][:].rearrange("p k s x -> p (k s x)"), HALVES * PAIR * NB)
+            width = SPANS * PAIR * NB
+            u_mx[pair] = mx_tiles("u", width, T // PAIR)
+            quantize(u_mx[pair], slice(0, width), u_turned[pair][:].rearrange("p q s x -> p (q s x)"))
 
-        state, h_grouped, h_mx = {}, {}, {}
+        state, h_values, h_mx = {}, {}, {}
+        real, imag, both = slice(0, NB), slice(NB, 2 * NB), slice(0, 2 * NB)
+        H_VALUES_BUFS = 5
+        H_MX_BUFS = 6
 
-        def project_in(g, pair, j):
-            if j == 0:
-                state[g, pair] = work.tile([P, PACK, PAIR, PARTS * NB], F32, name="state", bufs=6)
-            bank = psum.tile([P, PARTS, PAIR * NB], F32, name="bank", bufs=8)
-            for part in range(PARTS):
-                for kh in range(HALVES):
-                    matmul_mx(bank[:, part, :], w_mx["b", g, part, kh], slice(j * P, (j + 1) * P),
-                              u_mx[pair], slice(kh * PAIR * NB, (kh + 1) * PAIR * NB), kh == 0, kh == HALVES - 1)
-            col = PACK * g + j
-            nc.scalar.activation(out=state[g, pair][:, j].rearrange("p s (r b) -> p s r b", r=PARTS),
-                                 in_=bank[:].rearrange("p r (s b) -> p s r b", s=PAIR),
-                                 func=ACT.Copy, scale=gain[:, col:col + 1])
+        def project_in(g, pair):
+            tile = work.tile([P, PACK, PAIR, PARTS * NB], F32, name="state", bufs=6)
+            for j in range(PACK):
+                bank = psum.tile([P, PARTS, PAIR * NB], F32, name="bank", bufs=BANKS)
+                for part in range(PARTS):
+                    for q in range(SPANS):
+                        matmul_mx(bank[:, part, :], w_mx["b", g, part, q], slice(j * P, (j + 1) * P),
+                                  u_mx[pair], slice(q * PAIR * NB, (q + 1) * PAIR * NB), q == 0, q == SPANS - 1)
+                col = PACK * g + j
+                nc.scalar.activation(out=tile[:, j].rearrange("p s (a r) -> p s a r", a=PARTS),
+                                     in_=bank[:].rearrange("p a (s r) -> p s a r", s=PAIR),
+                                     func=ACT.Copy, scale=gain[:, col:col + 1])
+            state[g, pair] = tile
 
         def step_view(g, t):
             pair, s = divmod(t, PAIR)
             return state[g, pair][:, :, s, :]
 
-        def recur(g, t, terms=range(3)):
+        def add_term(g, t, to, frm, factor):
             old, new = step_view(g, t - 1), step_view(g, t)
-            re, im = slice(0, NB), slice(NB, 2 * NB)
-            table = ((slice(0, 2 * NB), slice(0, 2 * NB), lam[:, 1, :]), (re, im, li_neg[:]), (im, re, lam[:, 0, :]))
-            for term in terms:
-                to, frm, factor = table[term]
-                for j in range(PACK):
-                    col = PACK * g + j
-                    nc.vector.scalar_tensor_tensor(out=new[:, j, to], in0=old[:, j, frm], scalar=factor[:, col:col + 1],
-                                                   in1=new[:, j, to], op0=ALU.mult, op1=ALU.add)
+            for j in range(PACK):
+                col = PACK * g + j
+                nc.vector.scalar_tensor_tensor(out=new[:, j, to], in0=old[:, j, frm], scalar=factor[:, col:col + 1],
+                                               in1=new[:, j, to], op0=ALU.mult, op1=ALU.add)
 
-        def recur_on_tensor(t, js):
+        def add_own_term(g, t):
+            add_term(g, t, both, both, lr)
+
+        def add_cross_terms(g, t):
+            add_term(g, t, real, imag, li_neg[:])
+            add_term(g, t, imag, real, li)
+
+        def recur(g, t):
+            add_own_term(g, t)
+            add_cross_terms(g, t)
+
+        def cross_on_tensor(t, js):
             old, new = step_view(0, t - 1), step_view(0, t)
-            banks = []
+            banks = {}
             for j in js:
-                bank = psum.tile([P, PARTS * NB], F32, name="bank", bufs=8)
+                bank = psum.tile([P, PARTS * NB], F32, name="bank", bufs=BANKS)
                 nc.tensor.matmul(bank[:], lhsT=ident[:], rhs=new[:, j, :], start=True, stop=False)
-                for part in range(PARTS):
-                    other = 1 - part
-                    nc.tensor.matmul(bank[:, part * NB:(part + 1) * NB], lhsT=cross[:, part, j, :],
-                                     rhs=old[:, j, other * NB:(other + 1) * NB], start=False, stop=part == PARTS - 1)
-                banks.append(bank)
+                nc.tensor.matmul(bank[:, real], lhsT=cross[:, 0, j, :], rhs=old[:, j, imag], start=False, stop=False)
+                nc.tensor.matmul(bank[:, imag], lhsT=cross[:, 1, j, :], rhs=old[:, j, real], start=False, stop=True)
+                banks[j] = bank
             return banks
 
-        def update(t, js, banks):
+        def add_own_term_to_bank(t, banks, js):
             old, new = step_view(0, t - 1), step_view(0, t)
-            for j, bank in zip(js, banks):
-                nc.vector.scalar_tensor_tensor(out=new[:, j, :], in0=old[:, j, :], scalar=lam[:, 1, j:j + 1],
-                                               in1=bank[:], op0=ALU.mult, op1=ALU.add)
+            for j in js:
+                nc.vector.scalar_tensor_tensor(out=new[:, j, :], in0=old[:, j, :], scalar=lr[:, j:j + 1],
+                                               in1=banks[j][:], op0=ALU.mult, op1=ALU.add)
 
         def round_state(g, t):
-            tile = work.tile([P, PARTS * NB * PACK], BF16, name="h_grouped", bufs=4, align_bytes=64)
-            nc.scalar.copy(out=tile[:].rearrange("p (c i j) -> p c j i", i=RUN, j=PACK),
-                           in_=step_view(g, t).rearrange("p j (c i) -> p c j i", i=RUN))
-            h_grouped[g, t] = tile
+            tile = work.tile([P, PARTS * NB * PACK], BF16, name="h_values", bufs=H_VALUES_BUFS, align_bytes=64)
+            dst, src = interleave_views(tile[:], step_view(g, t))
+            nc.scalar.copy(out=dst, in_=src)
+            h_values[g, t] = tile
 
         def quantize_state(g, t):
-            h_mx[g, t] = quantize("h", 6, h_grouped[g, t][:], PARTS * NB)
+            h_mx[g, t] = mx_tiles("h", PARTS * NB, H_MX_BUFS)
+            quantize(h_mx[g, t], both, h_values[g, t][:])
 
         result, acc_out = {}, {}
 
-        def skip_term(t, half):
+        def skip_term(t):
             pair, s = divmod(t, PAIR)
-            bank = psum.tile([P, PACK, P], F32, name="bank", bufs=8)
-            rows = u_turned[pair][:, half, s, :].rearrange("p (b j) -> p j b", j=PACK)
-            for j in range(PACK):
-                nc.tensor.matmul(bank[:, j, :], lhsT=rows[:, j, :], rhs=d_diag[:, PACK * half + j, :],
-                                 start=True, stop=True)
-            tile = work.tile([P, KP], F32, name="result", bufs=8)
-            nc.scalar.copy(out=tile[:].rearrange("p (m j) -> p m j", j=PACK), in_=bank[:].rearrange("p j m -> p m j"))
-            result[t, half] = tile
+            for q in range(SPANS):
+                bank = psum.tile([P, PACK, P], F32, name="bank", bufs=BANKS)
+                features = u_turned[pair][:, q, s, :].rearrange("p (r j) -> p j r", j=PACK)
+                for j in range(PACK):
+                    nc.tensor.matmul(bank[:, j, :], lhsT=features[:, j, :], rhs=d_diag[:, PACK * q + j, :],
+                                     start=True, stop=True)
+                tile = work.tile([P, SPAN], F32, name="result", bufs=8)
+                nc.scalar.copy(out=tile[:].rearrange("p (m j) -> p m j", j=PACK),
+                               in_=bank[:].rearrange("p j m -> p m j"))
+                result[t, q] = tile
 
-        def project_out(t, groups):
-            for half in range(HALVES if 0 in groups else 0):
-                acc_out[t, half] = psum.tile([P, KP], F32, name="bank", bufs=8)
-            for g in groups:
-                for part in range(PARTS):
-                    for half in range(HALVES):
-                        matmul_mx(acc_out[t, half][:], h_mx[g, t], slice(part * NB, (part + 1) * NB),
-                                  w_mx["c", g, part, half], slice(0, KP),
-                                  g == 0 and part == 0, g == HALVES - 1 and part == PARTS - 1)
+        def project_out_group(t, g):
+            if g == 0:
+                for q in range(SPANS):
+                    acc_out[t, q] = psum.tile([P, SPAN], F32, name="bank", bufs=BANKS)
+            for part, cols in enumerate((real, imag)):
+                for q in range(SPANS):
+                    matmul_mx(acc_out[t, q][:], h_mx[g, t], cols, w_mx["c", g, part, q], slice(0, SPAN),
+                              g == 0 and part == 0, g == SPANS - 1 and part == PARTS - 1)
 
-        def finish(t, half, pieces=1):
-            tile, width = result[t, half], KP // pieces
-            for piece in range(pieces):
-                span = slice(piece * width, (piece + 1) * width)
-                nc.vector.tensor_tensor(out=tile[:, span], in0=acc_out[t, half][:, span], in1=tile[:, span], op=ALU.add)
-                nc.sync.dma_start(out=out[:, t, half * KP:(half + 1) * KP][:, span], in_=tile[:, span])
+        def project_out(t):
+            for g in range(SPANS):
+                project_out_group(t, g)
 
-        b_units = [("b", g, part, kh) for g in range(HALVES) for part in range(PARTS) for kh in range(HALVES)]
-        c_tiles = [(g, part) for g in range(HALVES) for part in range(PARTS)]
-        c_units = [("c", g, part, half) for g, part in c_tiles for half in range(HALVES)]
-        pending = []
+        def finish(t, q, cols=slice(0, SPAN)):
+            tile = result[t, q]
+            nc.vector.tensor_tensor(out=tile[:, cols], in0=acc_out[t, q][:, cols], in1=tile[:, cols], op=ALU.add)
+            nc.sync.dma_start(out=out[:, t, q * SPAN:(q + 1) * SPAN][:, cols], in_=tile[:, cols])
 
-        def prepare(unit, on_scalar=False):
-            interleave(unit, on_scalar)
-            flush()
-            pending.append(unit)
-
-        def flush():
-            for unit in pending:
-                quantize_weights(unit)
-            pending.clear()
-
-        def widen_tile(k):
-            for j in range(PACK):
-                widen_c(*c_tiles[k], j)
-
-        def project_pair(g, pair):
-            for j in range(PACK):
-                project_in(g, pair, j)
-
-        def turn_pair(pair):
-            for s in range(PAIR):
-                turn_u(PAIR * pair + s)
-
-        def skip_step(t):
-            for half in range(HALVES):
-                skip_term(t, half)
-
-        tile = work.tile([P, KP * PACK], BF16, name="grouped", bufs=4, align_bytes=64)
+        first_values = values_tile(b_blocks[0])[:].rearrange("p (s h m j) -> p h m j s", s=PACK, h=2, j=PACK)
         for piece in range(2):
-            nc.vector.tensor_copy(
-                out=tile[:].rearrange("p (s h m j) -> p h m j s", s=PACK, h=2, j=PACK)[:, piece],
-                in_=first_b[piece][:].rearrange("p j (m s) -> p m j s", s=PACK))
-        grouped[b_units[0]] = tile
-        quantize_weights(b_units[0])
-        turn_pair(0)
-        prepare(b_units[1])
+            nc.vector.tensor_copy(out=first_values[:, piece],
+                                  in_=first_b[piece][:].rearrange("p j (m s) -> p m j s", s=PACK))
+        quantize_block(b_blocks[0])
+        interleave(b_blocks[1])
         eigenvalues()
-        skip_step(0)
-        skip_step(1)
-        prepare(b_units[2])
+        quantize_block(b_blocks[1])
+        widen_c(0, 0)
+        prepare(b_blocks[2])
         load_b(1, 0, 0)
-        load_b(1, 0, 1)
-        quantize_u(0)
-        prepare(b_units[3])
-        load_b(1, 1, 0)
         load_c(0, 1)
-        nc.scalar.copy(out=gain[:], in_=gamma_sb)
-        nc.scalar.activation(out=cs_neg[:], in_=cs_sb, func=ACT.Copy, scale=-1.0)
-        widen_c(0, 0, 0)
-        turn_pair(1)
+        load_b(1, 0, 1)
         cross_matrices()
-        flush()
+        turn_u(0)
+        prepare(b_blocks[3])
+        quantize_waiting()
+        quantize_u(0)
+        load_b(1, 1, 0)
+        turn_u(1)
+        scalar_constants()
+        project_in(0, 0)
+        prepare(b_blocks[4])
         load_b(1, 1, 1)
         load_c(1, 0)
         load_u(2)
-        widen_c(0, 0, 1)
-        widen_c(0, 0, 2)
-        project_pair(0, 0)
         quantize_u(1)
-        prepare(b_units[4])
-        project_pair(0, 1)
-        widen_c(0, 0, 3)
+        project_in(0, 1)
         load_u(3)
         load_c(1, 1)
-        prepare(b_units[5])
+        prepare(b_blocks[5])
 
-        later = b_units[6:8] + c_units[0:4]
-        extra = {
-            0: [lambda: widen_tile(1)],
-            2: [lambda: project_pair(1, 0), lambda: widen_tile(2)],
-            4: [lambda: turn_pair(2), lambda: widen_tile(3)],
-        }
-        waiting = None
-        for i, unit in enumerate(later):
-            t, js = 1 + i // 2, range(2 * (i % 2), 2 * (i % 2) + 2)
-            half_step = (t, js, recur_on_tensor(t, js))
-            prepare(unit)
-            if waiting is not None:
-                update(*waiting)
-            waiting = half_step
-            for job in extra.get(i, []):
-                job()
-        prepare(c_units[4])
-        update(*waiting)
-        project_pair(1, 1)
-        prepare(c_units[5])
+        low, high = range(0, 2), range(2, PACK)
+        banks_1_low = cross_on_tensor(1, low)
+        prepare(b_blocks[6])
+        widen_c(0, 1)
+        banks_1_high = cross_on_tensor(1, high)
+        prepare(b_blocks[7])
+        add_own_term_to_bank(1, banks_1_low, low)
+        turn_u(2)
+        widen_c(1, 0)
+        banks_2_low = cross_on_tensor(2, low)
+        prepare(c_blocks[0])
+        add_own_term_to_bank(1, banks_1_high, high)
+        banks_2_high = cross_on_tensor(2, high)
+        prepare(c_blocks[1])
         quantize_u(2)
-        interleave(c_units[7], True)
-        recur(1, 1)
+        add_own_term_to_bank(2, banks_2_low, low)
+        banks_3_low = cross_on_tensor(3, low)
+        prepare(c_blocks[2])
+        add_own_term_to_bank(2, banks_2_high, high)
+        widen_c(1, 1)
+        banks_3_high = cross_on_tensor(3, high)
+        prepare(c_blocks[3])
+        add_own_term_to_bank(3, banks_3_low, low)
+        project_in(1, 0)
+        prepare(c_blocks[4])
+        add_own_term_to_bank(3, banks_3_high, high)
+        project_in(0, 2)
+        prepare(c_blocks[5])
+
+        banks_4 = cross_on_tensor(4, range(PACK))
         round_state(0, 0)
         round_state(1, 0)
-        prepare(c_units[6])
-        project_pair(0, 2)
-        quantize_weights(c_units[7])
-        flush()
+        project_in(1, 1)
+        recur(1, 1)
+        prepare(c_blocks[6])
+        prepare(c_blocks[7])
+        add_own_term_to_bank(4, banks_4, low)
+        quantize_waiting()
+        add_own_term_to_bank(4, banks_4, high)
+        turn_u(3)
         quantize_state(0, 0)
         quantize_state(1, 0)
-        turn_pair(3)
+        recur(0, 5)
         round_state(0, 1)
         round_state(1, 1)
-        project_out(0, range(HALVES))
+        round_state(0, 2)
+        skip_term(0)
+        project_out(0)
 
-        last = T - 1
-        for t in range(2, last):
+        pairs_left = {2: (0, 3), 3: (1, 2), 4: (1, 3)}
+        next_skip = 1
+        for t in range(2, LAST):
             recur(1, t)
             if t == 2:
                 quantize_u(3)
-            js = range(2 * (t % 2), 2 * (t % 2) + 2)
-            if t < T - PAIR:
-                for j in js:
-                    project_in(1, t // PAIR + 1, j)
-            if t < 4:
-                for j in js:
-                    project_in(0, 3, j)
+            if t in pairs_left:
+                project_in(*pairs_left[t])
+            round_state(1, t)
+            round_state(0, t + 1)
+            skip_until = t - 1 if t in pairs_left else t
+            for step in range(next_skip, skip_until + 1):
+                skip_term(step)
+            next_skip = skip_until + 1
+            if t in (3, 4):
+                recur(0, t + 3)
             quantize_state(0, t - 1)
             quantize_state(1, t - 1)
-            round_state(0, t)
-            round_state(1, t)
-            skip_step(t)
-            if t + 2 < T:
-                recur(0, t + 2)
-            for half in range(HALVES):
-                finish(t - 2, half)
-            project_out(t - 1, range(HALVES))
+            for q in range(SPANS):
+                finish(t - 2, q)
+            project_out(t - 1)
 
-        round_state(0, last)
-        quantize_state(0, last - 1)
-        for half in range(HALVES):
-            skip_term(last, half)
-        project_out(last - 1, [0])
-        finish(last - 2, 0)
-        recur(1, last, terms=[0])
-        quantize_state(1, last - 1)
-        quantize_state(0, last)
-        recur(1, last, terms=[1, 2])
-        project_out(last, [0])
-        project_out(last - 1, [1])
-        tile = work.tile([P, PARTS * NB * PACK], BF16, name="h_grouped", bufs=4, align_bytes=64)
-        codes, scales = mx_tiles("h", PARTS * NB, 6)
-        h_mx[1, last] = codes, scales
-        for part in range(PARTS):
-            words = slice(part * NB, (part + 1) * NB)
-            dst = tile[:, part * KP:(part + 1) * KP]
-            copy(part == 0, dst.rearrange("p (c i j) -> p c j i", i=RUN, j=PACK),
-                 step_view(1, last)[:, :, words].rearrange("p j (c i) -> p c j i", i=RUN))
-        for part in range(PARTS):
-            words = slice(part * NB, (part + 1) * NB)
-            nc.vector.quantize_mx(out=codes[:, words].bitcast(FP8X4), scales=scales[:, words],
-                                  in_=tile[:, part * KP:(part + 1) * KP])
-        finish(last - 2, 1)
-        project_out(last, [1])
-        for half in range(HALVES):
-            finish(last - 1, half)
-        finish(last, 0)
-        finish(last, 1, pieces=2)
+        quantize_state(0, LAST - 1)
+        skip_term(LAST)
+        project_out_group(LAST - 1, 0)
+        add_own_term(1, LAST)
+        quantize_state(1, LAST - 1)
+        quantize_state(0, LAST)
+        finish(LAST - 2, 0)
+        add_cross_terms(1, LAST)
+        project_out_group(LAST, 0)
+        project_out_group(LAST - 1, 1)
+        last_values = work.tile([P, PARTS * NB * PACK], BF16, name="h_values", bufs=H_VALUES_BUFS, align_bytes=64)
+        h_mx[1, LAST] = mx_tiles("h", PARTS * NB, H_MX_BUFS)
+        real_values, imag_values = last_values[:, 0:SPAN], last_values[:, SPAN:2 * SPAN]
+        dst_real, src_real = interleave_views(real_values, step_view(1, LAST)[:, :, real])
+        nc.scalar.copy(out=dst_real, in_=src_real)
+        dst_imag, src_imag = interleave_views(imag_values, step_view(1, LAST)[:, :, imag])
+        nc.vector.tensor_copy(out=dst_imag, in_=src_imag)
+        quantize(h_mx[1, LAST], real, real_values)
+        quantize(h_mx[1, LAST], imag, imag_values)
+        finish(LAST - 2, 1)
+        project_out_group(LAST, 1)
+        for q in range(SPANS):
+            finish(LAST - 1, q)
+        finish(LAST, 0)
+        finish(LAST, 1, slice(0, SPAN // 2))
+        finish(LAST, 1, slice(SPAN // 2, SPAN))

import math
from contextlib import ExitStack

import concourse.mybir as mybir
from concourse.masks import make_identity

NB, T, D, N = 128, 8, 1024, 1024
FLOPS = 2 * (NB * T) * D * (2 * N) + 2 * (NB * T) * (2 * N) * D

F32 = mybir.dt.float32
BF16 = mybir.dt.bfloat16
U32 = mybir.dt.uint32
U8 = mybir.dt.uint8
FP8 = mybir.dt.float8_e4m3fn
FP8X4 = mybir.dt.float8_e4m3fn_x4
ACT = mybir.ActivationFunctionType
ALU = mybir.AluOpType

P = 128
PACK = 4
SPAN = P * PACK
SPANS = 2
PARTS = 2
PAIR = 2
RUN = 4
COLS = SPANS * PACK
BANKS = 8
LAST = T - 1


def tile_linearrecurrentunitcomplexeightstep_kernel(tc, u, b, nu, theta, gamma, c_bytes, c_scale, d, out):
    nc = tc.nc
    with ExitStack() as ctx:
        const = ctx.enter_context(tc.tile_pool(name="const", bufs=1))
        work = ctx.enter_context(tc.tile_pool(name="work", bufs=1))
        psum = ctx.enter_context(tc.psum_pool(name="psum", bufs=1))
        ctx.enter_context(tc.manual_schedule())

        b_raw, c_raw, u_raw = {}, {}, {}

        def load_vector(queue, name, vec, dtype):
            tile = const.tile([P, SPANS, PACK], dtype, name=name)
            queue.dma_start(out=tile[:], in_=vec.rearrange("(q p j) -> p q j", p=P, j=PACK))
            return tile[:].rearrange("p q j -> p (q j)")

        def load_b(g, part, q):
            tile = work.tile([P, PACK, SPAN], BF16, name="b_raw", bufs=4)
            rows = b[part, q * SPAN:(q + 1) * SPAN, g * SPAN:(g + 1) * SPAN]
            nc.sync.dma_start(out=tile[:], in_=rows.rearrange("(p j) n -> p j n", j=PACK))
            b_raw[g, part, q] = tile

        def load_c(g, part):
            tile = work.tile([P, PACK, D], U8, name="c_raw", bufs=3)
            rows = c_bytes[part, g * SPAN:(g + 1) * SPAN, :]
            nc.sync.dma_start(out=tile[:], in_=rows.rearrange("(p j) f -> p j f", j=PACK))
            c_raw[g, part] = tile

        def load_u(pair):
            tile = work.tile([P, PAIR, D], BF16, name="u_raw", bufs=2)
            nc.sync.dma_start(out=tile[:], in_=u[:, PAIR * pair:PAIR * (pair + 1), :])
            u_raw[pair] = tile

        piece_cols = SPAN // 2
        first_b = []
        for piece in range(2):
            piece_tile = work.tile([P, PACK, piece_cols], BF16, name="b_first", bufs=2)
            piece_rows = b[0, 0:SPAN, piece * piece_cols:(piece + 1) * piece_cols]
            nc.sync.dma_start(out=piece_tile[:], in_=piece_rows.rearrange("(p j) n -> p j n", j=PACK))
            first_b.append(piece_tile)
        nu_sb = load_vector(nc.scalar, "nu_sb", nu, BF16)
        theta_sb = load_vector(nc.scalar, "theta_sb", theta, BF16)
        cs_sb = load_vector(nc.scalar, "cs_sb", c_scale.rearrange("o n z -> (o n z)"), F32)
        load_b(0, 0, 1)
        load_c(0, 0)
        load_b(0, 1, 0)
        load_u(0)
        load_b(0, 1, 1)
        load_u(1)
        gamma_sb = load_vector(nc.sync, "gamma_sb", gamma, BF16)
        d_sb = load_vector(nc.sync, "d_sb", d, BF16)

        ident = const.tile([P, P], F32, name="ident")
        make_identity(nc, ident[:])

        rate = const.tile([P, COLS], F32, name="rate")
        modulus = const.tile([P, COLS], F32, name="modulus")
        sin_cos = const.tile([P, 2, COLS], F32, name="sin_cos")
        li_lr = const.tile([P, 2, COLS], F32, name="li_lr")
        li_neg = const.tile([P, COLS], F32, name="li_neg")
        li, lr = li_lr[:, 0, :], li_lr[:, 1, :]
        cross = const.tile([P, PARTS, PACK, P], F32, name="cross")
        gain = const.tile([P, COLS], F32, name="gain")
        cs_neg = const.tile([P, COLS], F32, name="cs_neg")
        d_wide = const.tile([P, COLS], F32, name="d_wide")
        d_diag = const.tile([P, COLS, P], BF16, name="d_diag")

        nc.scalar.activation(out=rate[:], in_=nu_sb, func=ACT.Exp)
        nc.scalar.activation(out=modulus[:], in_=rate[:], func=ACT.Exp, scale=-1.0)
        nc.scalar.activation(out=sin_cos[:, 0, :], in_=theta_sb, func=ACT.Sin)
        nc.scalar.activation(out=sin_cos[:, 1, :], in_=theta_sb, func=ACT.Sin, scale=-1.0, bias=math.pi / 2)

        def eigenvalues():
            nc.vector.tensor_tensor(out=li_lr[:], in0=sin_cos[:],
                                    in1=modulus[:].unsqueeze(1).to_broadcast([P, 2, COLS]), op=ALU.mult)
            nc.vector.scalar_tensor_tensor(out=li_neg[:], in0=sin_cos[:, 0, :], scalar=-1.0, in1=modulus[:],
                                           op0=ALU.mult, op1=ALU.mult)

        def cross_matrices():
            for part, factor in enumerate((li_neg[:], li)):
                for j in range(PACK):
                    nc.vector.tensor_scalar(out=cross[:, part, j, :], in0=ident[:], scalar1=factor[:, j:j + 1],
                                            scalar2=None, op0=ALU.mult)

        def scalar_constants():
            nc.scalar.copy(out=gain[:], in_=gamma_sb)
            nc.scalar.activation(out=cs_neg[:], in_=cs_sb, func=ACT.Copy, scale=-1.0)
            nc.scalar.copy(out=d_wide[:], in_=d_sb)
            for col in range(COLS):
                nc.scalar.activation(out=d_diag[:, col, :], in_=ident[:], func=ACT.Copy, scale=d_wide[:, col:col + 1])

        def mx_tiles(name, width, bufs):
            codes = work.tile([P, width], U32, name=name + "_codes", bufs=bufs, align_bytes=64)
            scales = work.tile([P, width], U8, name=name + "_scales", bufs=bufs, align_bytes=64)
            return codes, scales

        def quantize(operand, cols, values):
            codes, scales = operand
            nc.vector.quantize_mx(out=codes[:, cols].bitcast(FP8X4), scales=scales[:, cols], in_=values)

        def matmul_mx(acc, lhs, lhs_cols, rhs, rhs_cols, start, stop):
            nc.tensor.matmul_mx(out=acc, lhsT=lhs[0][:, lhs_cols].bitcast(FP8X4), lhsT_scale=lhs[1][:, lhs_cols],
                                rhs=rhs[0][:, rhs_cols].bitcast(FP8X4), rhs_scale=rhs[1][:, rhs_cols],
                                start=start, stop=stop)

        def interleave_views(dst, src):
            return (dst.rearrange("p (c i j) -> p c j i", i=RUN, j=PACK),
                    src.rearrange("p j (c i) -> p c j i", i=RUN))

        b_blocks = [("b", g, part, q) for g in range(SPANS) for part in range(PARTS) for q in range(SPANS)]
        c_blocks = [("c", g, part, q) for g in range(SPANS) for part in range(PARTS) for q in range(SPANS)]
        c_wide, w_values, w_mx, unquantized = {}, {}, {}, []

        def widen_c(g, part):
            tile = work.tile([P, PACK, D], BF16, name="c_wide", bufs=3)
            factor = (cs_sb, cs_neg[:])[part]
            for j in range(PACK):
                col = PACK * g + j
                nc.scalar.activation(out=tile[:, j, :], in_=c_raw[g, part][:, j, :].bitcast(FP8),
                                     func=ACT.Copy, scale=factor[:, col:col + 1])
            c_wide[g, part] = tile

        def values_tile(block):
            w_values[block] = work.tile([P, SPAN * PACK], BF16, name="w_values", bufs=4, align_bytes=64)
            return w_values[block]

        def interleave(block):
            kind, g, part, q = block
            tile = values_tile(block)
            if kind == "b":
                dst = tile[:].rearrange("p (s m j) -> p m j s", s=PACK, j=PACK)
                src = b_raw[g, part, q][:].rearrange("p j (m s) -> p m j s", s=PACK)
            else:
                dst, src = interleave_views(tile[:], c_wide[g, part][:, :, q * SPAN:(q + 1) * SPAN])
            nc.vector.tensor_copy(out=dst, in_=src)

        def quantize_block(block):
            w_mx[block] = mx_tiles("w", SPAN, len(b_blocks) + len(c_blocks))
            quantize(w_mx[block], slice(0, SPAN), w_values[block][:])

        def quantize_waiting():
            for block in unquantized:
                quantize_block(block)
            unquantized.clear()

        def prepare(block):
            interleave(block)
            quantize_waiting()
            unquantized.append(block)

        u_turned, u_mx = {}, {}

        def turn_u(pair):
            tile = work.tile([P, SPANS, PAIR, NB * PACK], BF16, name="u_turned", bufs=T // PAIR, align_bytes=64)
            for s in range(PAIR):
                words = u_raw[pair][:, s, :].bitcast(F32)
                bank = psum.tile([P, SPANS, 2, NB], F32, name="bank", bufs=BANKS)
                for q in range(SPANS):
                    for w in range(2):
                        nc.tensor.transpose(bank[:, q, w, :], words[:, 2 * P * q + w:2 * P * (q + 1):2], ident[:])
                nc.scalar.copy(out=tile[:, :, s, :].bitcast(F32).rearrange("p q (r w) -> p q r w", w=2),
                               in_=bank[:].rearrange("p q w r -> p q r w"))
            u_turned[pair] = tile

        def quantize_u(pair):
            width = SPANS * PAIR * NB
            u_mx[pair] = mx_tiles("u", width, T // PAIR)
            quantize(u_mx[pair], slice(0, width), u_turned[pair][:].rearrange("p q s x -> p (q s x)"))

        state, h_values, h_mx = {}, {}, {}
        real, imag, both = slice(0, NB), slice(NB, 2 * NB), slice(0, 2 * NB)
        H_VALUES_BUFS = 5
        H_MX_BUFS = 6

        def project_in(g, pair):
            tile = work.tile([P, PACK, PAIR, PARTS * NB], F32, name="state", bufs=6)
            for j in range(PACK):
                bank = psum.tile([P, PARTS, PAIR * NB], F32, name="bank", bufs=BANKS)
                for part in range(PARTS):
                    for q in range(SPANS):
                        matmul_mx(bank[:, part, :], w_mx["b", g, part, q], slice(j * P, (j + 1) * P),
                                  u_mx[pair], slice(q * PAIR * NB, (q + 1) * PAIR * NB), q == 0, q == SPANS - 1)
                col = PACK * g + j
                nc.scalar.activation(out=tile[:, j].rearrange("p s (a r) -> p s a r", a=PARTS),
                                     in_=bank[:].rearrange("p a (s r) -> p s a r", s=PAIR),
                                     func=ACT.Copy, scale=gain[:, col:col + 1])
            state[g, pair] = tile

        def step_view(g, t):
            pair, s = divmod(t, PAIR)
            return state[g, pair][:, :, s, :]

        def add_term(g, t, to, frm, factor):
            old, new = step_view(g, t - 1), step_view(g, t)
            for j in range(PACK):
                col = PACK * g + j
                nc.vector.scalar_tensor_tensor(out=new[:, j, to], in0=old[:, j, frm], scalar=factor[:, col:col + 1],
                                               in1=new[:, j, to], op0=ALU.mult, op1=ALU.add)

        def add_own_term(g, t):
            add_term(g, t, both, both, lr)

        def add_cross_terms(g, t):
            add_term(g, t, real, imag, li_neg[:])
            add_term(g, t, imag, real, li)

        def recur(g, t):
            add_own_term(g, t)
            add_cross_terms(g, t)

        def cross_on_tensor(t, js):
            old, new = step_view(0, t - 1), step_view(0, t)
            banks = {}
            for j in js:
                bank = psum.tile([P, PARTS * NB], F32, name="bank", bufs=BANKS)
                nc.tensor.matmul(bank[:], lhsT=ident[:], rhs=new[:, j, :], start=True, stop=False)
                nc.tensor.matmul(bank[:, real], lhsT=cross[:, 0, j, :], rhs=old[:, j, imag], start=False, stop=False)
                nc.tensor.matmul(bank[:, imag], lhsT=cross[:, 1, j, :], rhs=old[:, j, real], start=False, stop=True)
                banks[j] = bank
            return banks

        def add_own_term_to_bank(t, banks, js):
            old, new = step_view(0, t - 1), step_view(0, t)
            for j in js:
                nc.vector.scalar_tensor_tensor(out=new[:, j, :], in0=old[:, j, :], scalar=lr[:, j:j + 1],
                                               in1=banks[j][:], op0=ALU.mult, op1=ALU.add)

        def round_state(g, t):
            tile = work.tile([P, PARTS * NB * PACK], BF16, name="h_values", bufs=H_VALUES_BUFS, align_bytes=64)
            dst, src = interleave_views(tile[:], step_view(g, t))
            nc.scalar.copy(out=dst, in_=src)
            h_values[g, t] = tile

        def quantize_state(g, t):
            h_mx[g, t] = mx_tiles("h", PARTS * NB, H_MX_BUFS)
            quantize(h_mx[g, t], both, h_values[g, t][:])

        result, acc_out = {}, {}

        def skip_term(t):
            pair, s = divmod(t, PAIR)
            for q in range(SPANS):
                bank = psum.tile([P, PACK, P], F32, name="bank", bufs=BANKS)
                features = u_turned[pair][:, q, s, :].rearrange("p (r j) -> p j r", j=PACK)
                for j in range(PACK):
                    nc.tensor.matmul(bank[:, j, :], lhsT=features[:, j, :], rhs=d_diag[:, PACK * q + j, :],
                                     start=True, stop=True)
                tile = work.tile([P, SPAN], F32, name="result", bufs=8)
                nc.scalar.copy(out=tile[:].rearrange("p (m j) -> p m j", j=PACK),
                               in_=bank[:].rearrange("p j m -> p m j"))
                result[t, q] = tile

        def project_out_group(t, g):
            if g == 0:
                for q in range(SPANS):
                    acc_out[t, q] = psum.tile([P, SPAN], F32, name="bank", bufs=BANKS)
            for part, cols in enumerate((real, imag)):
                for q in range(SPANS):
                    matmul_mx(acc_out[t, q][:], h_mx[g, t], cols, w_mx["c", g, part, q], slice(0, SPAN),
                              g == 0 and part == 0, g == SPANS - 1 and part == PARTS - 1)

        def project_out(t):
            for g in range(SPANS):
                project_out_group(t, g)

        def finish(t, q, cols=slice(0, SPAN)):
            tile = result[t, q]
            nc.vector.tensor_tensor(out=tile[:, cols], in0=acc_out[t, q][:, cols], in1=tile[:, cols], op=ALU.add)
            nc.sync.dma_start(out=out[:, t, q * SPAN:(q + 1) * SPAN][:, cols], in_=tile[:, cols])

        first_values = values_tile(b_blocks[0])[:].rearrange("p (s h m j) -> p h m j s", s=PACK, h=2, j=PACK)
        for piece in range(2):
            nc.vector.tensor_copy(out=first_values[:, piece],
                                  in_=first_b[piece][:].rearrange("p j (m s) -> p m j s", s=PACK))
        quantize_block(b_blocks[0])
        interleave(b_blocks[1])
        eigenvalues()
        quantize_block(b_blocks[1])
        widen_c(0, 0)
        prepare(b_blocks[2])
        load_b(1, 0, 0)
        load_c(0, 1)
        load_b(1, 0, 1)
        cross_matrices()
        turn_u(0)
        prepare(b_blocks[3])
        quantize_waiting()
        quantize_u(0)
        load_b(1, 1, 0)
        turn_u(1)
        scalar_constants()
        project_in(0, 0)
        prepare(b_blocks[4])
        load_b(1, 1, 1)
        load_c(1, 0)
        load_u(2)
        quantize_u(1)
        project_in(0, 1)
        load_u(3)
        load_c(1, 1)
        prepare(b_blocks[5])

        low, high = range(0, 2), range(2, PACK)
        banks_1_low = cross_on_tensor(1, low)
        prepare(b_blocks[6])
        widen_c(0, 1)
        banks_1_high = cross_on_tensor(1, high)
        prepare(b_blocks[7])
        add_own_term_to_bank(1, banks_1_low, low)
        turn_u(2)
        widen_c(1, 0)
        banks_2_low = cross_on_tensor(2, low)
        prepare(c_blocks[0])
        add_own_term_to_bank(1, banks_1_high, high)
        banks_2_high = cross_on_tensor(2, high)
        prepare(c_blocks[1])
        quantize_u(2)
        add_own_term_to_bank(2, banks_2_low, low)
        banks_3_low = cross_on_tensor(3, low)
        prepare(c_blocks[2])
        add_own_term_to_bank(2, banks_2_high, high)
        widen_c(1, 1)
        banks_3_high = cross_on_tensor(3, high)
        prepare(c_blocks[3])
        add_own_term_to_bank(3, banks_3_low, low)
        project_in(1, 0)
        prepare(c_blocks[4])
        add_own_term_to_bank(3, banks_3_high, high)
        project_in(0, 2)
        prepare(c_blocks[5])

        banks_4 = cross_on_tensor(4, range(PACK))
        round_state(0, 0)
        round_state(1, 0)
        project_in(1, 1)
        recur(1, 1)
        prepare(c_blocks[6])
        prepare(c_blocks[7])
        add_own_term_to_bank(4, banks_4, low)
        quantize_waiting()
        add_own_term_to_bank(4, banks_4, high)
        turn_u(3)
        quantize_state(0, 0)
        quantize_state(1, 0)
        recur(0, 5)
        round_state(0, 1)
        round_state(1, 1)
        round_state(0, 2)
        skip_term(0)
        project_out(0)

        pairs_left = {2: (0, 3), 3: (1, 2), 4: (1, 3)}
        next_skip = 1
        for t in range(2, LAST):
            recur(1, t)
            if t == 2:
                quantize_u(3)
            if t in pairs_left:
                project_in(*pairs_left[t])
            round_state(1, t)
            round_state(0, t + 1)
            skip_until = t - 1 if t in pairs_left else t
            for step in range(next_skip, skip_until + 1):
                skip_term(step)
            next_skip = skip_until + 1
            if t in (3, 4):
                recur(0, t + 3)
            quantize_state(0, t - 1)
            quantize_state(1, t - 1)
            for q in range(SPANS):
                finish(t - 2, q)
            project_out(t - 1)

        quantize_state(0, LAST - 1)
        skip_term(LAST)
        project_out_group(LAST - 1, 0)
        add_own_term(1, LAST)
        quantize_state(1, LAST - 1)
        quantize_state(0, LAST)
        finish(LAST - 2, 0)
        add_cross_terms(1, LAST)
        project_out_group(LAST, 0)
        project_out_group(LAST - 1, 1)
        last_values = work.tile([P, PARTS * NB * PACK], BF16, name="h_values", bufs=H_VALUES_BUFS, align_bytes=64)
        h_mx[1, LAST] = mx_tiles("h", PARTS * NB, H_MX_BUFS)
        real_values, imag_values = last_values[:, 0:SPAN], last_values[:, SPAN:2 * SPAN]
        dst_real, src_real = interleave_views(real_values, step_view(1, LAST)[:, :, real])
        nc.scalar.copy(out=dst_real, in_=src_real)
        dst_imag, src_imag = interleave_views(imag_values, step_view(1, LAST)[:, :, imag])
        nc.vector.tensor_copy(out=dst_imag, in_=src_imag)
        quantize(h_mx[1, LAST], real, real_values)
        quantize(h_mx[1, LAST], imag, imag_values)
        finish(LAST - 2, 1)
        project_out_group(LAST, 1)
        for q in range(SPANS):
            finish(LAST - 1, q)
        finish(LAST, 0)
        finish(LAST, 1, slice(0, SPAN // 2))
        finish(LAST, 1, slice(SPAN // 2, SPAN))
